import numpy as np
import ml_dtypes


def mxq(x, axis, fmt="e4m3"):
    dtype, down = {"e4m3": (ml_dtypes.float8_e4m3fn, 7), "e5m2": (ml_dtypes.float8_e5m2, 14)}[fmt]
    v = np.moveaxis(np.asarray(x, np.float32).astype(ml_dtypes.bfloat16).astype(np.float64), axis, -1)
    blocks = v.reshape(v.shape[:-1] + (-1, 32))
    amax = np.abs(blocks).max(-1, keepdims=True)
    byte = np.maximum(np.where(amax > 0, np.frexp(amax)[1] - 1 + 127, 0) - down, 1)
    scale = np.exp2(byte - 127.0)
    codes = (blocks / scale).astype(np.float32).astype(dtype).astype(np.float64)
    return np.moveaxis((codes * scale).reshape(v.shape), -1, axis)


WIDE = False


def mx_kscale(k):
    if not WIDE:
        return np.ones(k)
    levels = np.array([10, -10, 5, -5, 0])
    if k % 512:
        return np.exp2(np.random.permutation(np.resize(levels, k // 32))).repeat(32)
    a = np.empty((k // 512, 16))
    for p in range(k // 512):
        a[p, :8] = np.random.permutation(np.resize(levels, 8))
        for g in range(8):
            far = levels[np.abs(levels - a[p, g]) >= 10]
            a[p, g + 8] = far[np.random.randint(len(far))]
    return np.exp2(a.ravel()).repeat(32)


def f64(x):
    return np.asarray(x).astype(np.float64)


def striped(idx):
    return np.tile(idx.reshape(-1, 16).T, (8, 1)).astype(np.uint16)


def unstriped(offs):
    return offs[:16].T.reshape(-1).astype(np.int64)


E2M1 = np.array([0.0, 0.5, 1.0, 1.5, 2.0, 3.0, 4.0, 6.0, -0.0, -0.5, -1.0, -1.5, -2.0, -3.0, -4.0, -6.0])


def pack_weight(w, fmt):
    k, n = w.shape
    w = f64(np.asarray(w, np.float32).astype(ml_dtypes.bfloat16)).reshape(k // 32, 32, n)
    amax = np.abs(w).max(1)
    if fmt == "e4m3":
        byte = np.frexp(amax)[1] - 1 + 127 - 7
    else:
        mant, ex = np.frexp(amax / 6.0)
        byte = np.where(mant > 0.5, ex, ex - 1) + 127
    byte = np.clip(np.where(amax > 0, byte, 1), 1, 254)
    scaled = (w * np.exp2(127.0 - byte)[:, None, :]).reshape(k, n).astype(np.float32)
    by_word = np.ascontiguousarray(scaled.reshape(k // 512, 128, 4, n).transpose(0, 1, 3, 2))
    if fmt == "e4m3":
        words = by_word.astype(ml_dtypes.float8_e4m3fn).view(np.uint8)
    else:
        c = by_word.astype(ml_dtypes.float4_e2m1fn).view(np.uint8) & 0xF
        words = (c[..., 0::2] | (c[..., 1::2] << 4)).reshape(k // 512, 128, 2 * n)
    return np.ascontiguousarray(words), np.ascontiguousarray(byte.astype(np.uint8).reshape(k // 512, 16, n))


def unpack_weight(words, scales, fmt):
    g, _, n = scales.shape
    words = np.ascontiguousarray(words).reshape(g, 128, n, -1)
    if fmt == "e4m3":
        vals = words.view(ml_dtypes.float8_e4m3fn).astype(np.float64)
    else:
        nib = np.empty((g, 128, n, 4), np.uint8)
        nib[..., 0::2] = words & 0xF
        nib[..., 1::2] = words >> 4
        vals = E2M1[nib]
    vals = vals * np.repeat(np.exp2(scales.astype(np.float64) - 127.0), 8, axis=1)[..., None]
    return vals.transpose(0, 1, 3, 2).reshape(g * 512, n)


K, M, T, S = 512, 128, 4096, 2048


def setup_inputs():
    n = np.random.standard_normal
    s = mx_kscale(K)[:, None]
    s2 = mx_kscale(512)[:, None]
    v = pack_weight(n((K, T)) * s, "e4m3")
    p_w4 = pack_weight(n((K, M)) / np.sqrt(K) / s, "e2m1")
    return {
        "tab_words": v[0],
        "tab_scales": v[1],
        "w4_words": p_w4[0],
        "w4_scales": p_w4[1],
        "c": (n((512, S)) * s2).astype(np.float32),
        "u": (n((512, M)) / np.sqrt(512) / s2).astype(np.float32),
        "gT": n((M, T)).astype(np.float32),
        "b": (0.3 * n(128)).astype(np.float32),
        "offs": striped(np.random.permutation(T)[:S]),
    }


def reference(tab_words, tab_scales, w4_words, w4_scales, c, u, gT, b, offs):
    tab_ = unpack_weight(tab_words, tab_scales, "e4m3")[:, unstriped(offs)]
    w4_ = unpack_weight(w4_words, w4_scales, "e2m1")
    c_ = mxq(f64(c), 0, "e4m3")
    u_ = mxq(f64(u), 0, "e4m3")
    y = w4_.T @ tab_ + u_.T @ c_
    return (y + f64(b)[:, None]) * f64(gT)[:, unstriped(offs)]

@@ -1,0 +1,197 @@
+from contextlib import ExitStack
+
+import concourse.mybir as mybir
+
+K, M, T, S = 512, 128, 4096, 2048
+FLOPS = 2 * 2 * K * M * S
+
+F32 = mybir.dt.float32
+BF16 = mybir.dt.bfloat16
+I32 = mybir.dt.int32
+U32 = mybir.dt.uint32
+U16 = mybir.dt.uint16
+U8 = mybir.dt.uint8
+FP8X4 = mybir.dt.float8_e4m3fn_x4
+FP4X4 = mybir.dt.float4_e2m1fn_x4
+ADD = mybir.AluOpType.add
+MULT = mybir.AluOpType.mult
+IDENTITY = mybir.ActivationFunctionType.Identity
+
+P = 128
+PACK = 4
+PER_COL = 16
+
+CHUNKS = [(512, 0, 512, 512, True), (512, 0, 512, 512, False), (512, 0, 512, 512, False), (256, 256, 128, 256, False), (256, 0, 128, 256, False)]
+GATE_PIECE = 512
+
+
+def tile_list_tabgate_bias_kernel(tc, tab_words, tab_scales, w4_words, w4_scales, c, u, gT, b, offs, out):
+    nc = tc.nc
+    with ExitStack() as ctx:
+        keep = ctx.enter_context(tc.tile_pool(name="keep", bufs=1))
+        psum = ctx.enter_context(tc.psum_pool(name="psum", bufs=1))
+
+        offsets = keep.tile([P, S // PER_COL], U16, name="offsets")
+        tab_plane = keep.tile([P, T // 4], I32, name="tab_plane", align_bytes=64)
+        w4_plane = keep.tile([P, M // 4], I32, name="w4_plane", align_bytes=64)
+        tab_codes = keep.tile([P, T], I32, name="tab_codes", align_bytes=64)
+        w4_codes = keep.tile([P, M // 2], I32, name="w4_codes", align_bytes=64)
+        u_raw = keep.tile([P, PACK, M], F32, name="u_raw")
+        bias = keep.tile([P, 1], F32, name="bias")
+        gates = keep.tile([P, T], F32, name="gates")
+        starts = [sum(ch[0] for ch in CHUNKS[:i]) for i in range(len(CHUNKS))]
+        c_raw = [keep.tile([P, PACK, ch[0]], F32, name="c_raw%d" % i) for i, ch in enumerate(CHUNKS)]
+        c_rows = c.rearrange("(p t) j -> p t j", t=PACK)
+
+        def load_c(i):
+            nc.sync.dma_start(out=c_raw[i][:], in_=c_rows[:, :, starts[i] : starts[i] + CHUNKS[i][0]])
+
+        def load_plane(queue, plane, scale_rows):
+            rows = scale_rows[0].bitcast(I32)
+            for r in range(4):
+                queue.dma_start(out=plane[r:P:32, :], in_=rows[r:16:4, :])
+
+        nc.vector.memset(tab_plane[:], 0)
+        nc.vector.memset(w4_plane[:], 0)
+
+        def ld_offs():
+            nc.sync.dma_start(offsets[:], offs)
+
+        def ld_u():
+            nc.sync.dma_start(out=u_raw[:], in_=u.rearrange("(p t) n -> p t n", t=PACK))
+
+        def ld_w4(lo, hi):
+            nc.sync.dma_start(out=w4_codes[lo:hi, :], in_=w4_words[0].bitcast(I32)[lo:hi, :])
+
+        def ld_b(queue):
+            with nc.allow_non_contiguous_dma(reason="one bias value a partition"):
+                queue.dma_start(out=bias[:], in_=b.rearrange("(p o) -> p o", o=1))
+
+        def ld_words():
+            nc.sync.dma_start(out=tab_codes[:], in_=tab_words[0].rearrange("p t i -> p (t i)").bitcast(I32))
+
+        def ld_gates():
+            nc.sync.dma_start(out=gates[:], in_=gT)
+
+        ld_offs()
+        ld_u()
+        ld_w4(0, 96)
+        load_plane(nc.sync, tab_plane, tab_scales)
+        ld_words()
+        load_c(0)
+        ld_w4(96, 128)
+        load_plane(nc.sync, w4_plane, w4_scales)
+        ld_b(nc.sync)
+        ld_gates()
+        for i in range(1, len(CHUNKS)):
+            load_c(i)
+
+        def cast(engine_copy, grouped, raw, lo, hi):
+            engine_copy(
+                out=grouped[:, lo:hi, :].rearrange("p (a i) t -> p a t i", i=4),
+                in_=raw[:, :, lo:hi].rearrange("p t (a i) -> p a t i", i=4),
+            )
+
+        def quantise(codes, plane, grouped, lo, hi, at):
+            nc.vector.quantize_mx(
+                out=codes[:, at + lo : at + hi].bitcast(FP8X4),
+                scales=plane[:, at + lo : at + hi],
+                in_=grouped[:, lo:hi, :].rearrange("p j t -> p (j t)"),
+            )
+
+        picked_plane = keep.tile([P, S], U8, name="picked_plane", align_bytes=64)
+        picked_codes = keep.tile([P, S], U32, name="picked_codes", align_bytes=64)
+        nc.vector.tensor_copy(picked_plane[:], tab_plane[:].bitcast(U8).indirect(offsets[:]))
+        nc.vector.tensor_copy(picked_codes[:], tab_codes[:].bitcast(U32).indirect(offsets[:]))
+
+        u_grouped = keep.tile([P, M, PACK], BF16, name="u_grouped", align_bytes=64)
+        u_codes = keep.tile([P, M], U32, name="u_codes", align_bytes=64)
+        u_plane = keep.tile([P, M], U8, name="u_plane", align_bytes=64)
+        cast(nc.scalar.copy, u_grouped, u_raw, 0, M)
+        quantise(u_codes, u_plane, u_grouped, 0, M, 0)
+
+        c_codes = keep.tile([P, S], U32, name="c_codes", align_bytes=64)
+        c_plane = keep.tile([P, S], U8, name="c_plane", align_bytes=64)
+        picked_gates = keep.tile([P, S], F32, name="picked_gates")
+        banks = {}
+
+        def table_passes(i):
+            width, n = CHUNKS[i][0], CHUNKS[i][2]
+            for lo in range(starts[i], starts[i] + width, n):
+                banks[lo] = psum.tile([P, n], F32, name="bank%d" % lo)
+                nc.tensor.matmul_mx(
+                    out=banks[lo][:],
+                    lhsT=w4_codes[:].bitcast(FP4X4),
+                    lhsT_scale=w4_plane[:].bitcast(U8),
+                    rhs=picked_codes[:, lo : lo + n].bitcast(FP8X4),
+                    rhs_scale=picked_plane[:, lo : lo + n],
+                    start=True,
+                    stop=False,
+                )
+
+        summed = {}
+
+        def front(i):
+            width, on_vector, n, q, fused = CHUNKS[i]
+            at = starts[i]
+            grouped = keep.tile([P, width, PACK], BF16, name="grouped%d" % i, align_bytes=64)
+            if on_vector > 0:
+                cast(nc.vector.tensor_copy, grouped, c_raw[i], 0, on_vector)
+            if on_vector < width:
+                cast(nc.scalar.copy, grouped, c_raw[i], on_vector, width)
+            for lo in range(0, width, q):
+                quantise(c_codes, c_plane, grouped, lo, lo + q, at)
+            for lo in range(at, at + width, n):
+                nc.tensor.matmul_mx(
+                    out=banks[lo][:],
+                    lhsT=u_codes[:].bitcast(FP8X4),
+                    lhsT_scale=u_plane[:],
+                    rhs=c_codes[:, lo : lo + n].bitcast(FP8X4),
+                    rhs_scale=c_plane[:, lo : lo + n],
+                    start=False,
+                    stop=True,
+                )
+            if fused:
+                summed[i] = keep.tile([P, width], F32, name="summed%d" % i)
+                for lo in range(at, at + width, n):
+                    nc.scalar.activation(out=summed[i][:, lo - at : lo - at + n], in_=banks[lo][:], func=IDENTITY, bias=bias[:])
+
+        def back(i):
+            width, on_vector, n, q, fused = CHUNKS[i]
+            at = starts[i]
+            result = keep.tile([P, width], F32, name="result%d" % i)
+            if fused:
+                window = gates[:].indirect(offsets[:, at // PER_COL : (at + width) // PER_COL])
+                nc.vector.tensor_tensor(result[:], window, summed[i][:], MULT)
+            else:
+                for lo in range(at, at + width, n):
+                    nc.vector.scalar_tensor_tensor(
+                        out=result[:, lo - at : lo - at + n],
+                        in0=banks[lo][:],
+                        scalar=bias[:],
+                        in1=picked_gates[:, lo : lo + n],
+                        op0=ADD,
+                        op1=MULT,
+                    )
+            nc.sync.dma_start(out=out[:, at : at + width], in_=result[:])
+
+        def pick_gates(lo):
+            window = gates[:].indirect(offsets[:, lo // PER_COL : (lo + GATE_PIECE) // PER_COL])
+            nc.vector.tensor_copy(picked_gates[:, lo : lo + GATE_PIECE], window)
+
+        table_passes(0)
+        front(0)
+        for i in range(1, len(CHUNKS)):
+            table_passes(i)
+        pick_gates(512)
+        back(0)
+        pick_gates(1024)
+        pick_gates(1536)
+        front(1)
+        back(1)
+        front(2)
+        front(3)
+        front(4)
+        back(2)
+        back(3)
+        back(4)

@@ -21,8 +21,8 @@ P = 128
 PACK = 4
 PER_COL = 16
 
-CHUNKS = [(512, 0, 512, 512, True), (512, 0, 512, 512, False), (512, 0, 512, 512, False), (256, 256, 128, 256, False), (256, 0, 128, 256, False)]
-GATE_PIECE = 512
+CHUNKS = [(1024, 512, 512, 512, False), (512, 128, 512, 512, False), (256, 0, 128, 256, False), (256, 128, 128, 128, False)]
+GATE_PIECE = 2048
 
 
 def tile_list_tabgate_bias_kernel(tc, tab_words, tab_scales, w4_words, w4_scales, c, u, gT, b, offs, out):
@@ -78,12 +78,11 @@ def tile_list_tabgate_bias_kernel(tc, tab_words, tab_scales, w4_words, w4_scales
         ld_w4(0, 96)
         load_plane(nc.sync, tab_plane, tab_scales)
         ld_words()
-        load_c(0)
+        ld_gates()
         ld_w4(96, 128)
         load_plane(nc.sync, w4_plane, w4_scales)
         ld_b(nc.sync)
-        ld_gates()
-        for i in range(1, len(CHUNKS)):
+        for i in range(len(CHUNKS)):
             load_c(i)
 
         def cast(engine_copy, grouped, raw, lo, hi):
@@ -179,19 +178,10 @@ def tile_list_tabgate_bias_kernel(tc, tab_words, tab_scales, w4_words, w4_scales
             window = gates[:].indirect(offsets[:, lo // PER_COL : (lo + GATE_PIECE) // PER_COL])
             nc.vector.tensor_copy(picked_gates[:, lo : lo + GATE_PIECE], window)
 
-        table_passes(0)
-        front(0)
-        for i in range(1, len(CHUNKS)):
+        for i in range(len(CHUNKS)):
             table_passes(i)
-        pick_gates(512)
-        back(0)
-        pick_gates(1024)
-        pick_gates(1536)
-        front(1)
-        back(1)
-        front(2)
-        front(3)
-        front(4)
-        back(2)
-        back(3)
-        back(4)
+        pick_gates(0)
+        for i in range(len(CHUNKS)):
+            front(i)
+        for i in range(len(CHUNKS)):
+            back(i)

@@ -15,14 +15,23 @@ FP8X4 = mybir.dt.float8_e4m3fn_x4
 FP4X4 = mybir.dt.float4_e2m1fn_x4
 ADD = mybir.AluOpType.add
 MULT = mybir.AluOpType.mult
-IDENTITY = mybir.ActivationFunctionType.Identity
 
 P = 128
 PACK = 4
 PER_COL = 16
 
-CHUNKS = [(1024, 512, 512, 512, False), (512, 128, 512, 512, False), (256, 0, 128, 256, False), (256, 128, 128, 128, False)]
-GATE_PIECE = 2048
+CHUNKS = [(256, 0), (256, 0), (256, 0), (256, 128), (256, 0), (256, 128), (256, 0), (128, 0), (128, 0)]
+EARLY = 0
+GROUPS = [[0, 1], [2, 3], [4], [5], [6], [7], [8]]
+
+
+def pieces(width):
+    out, lo = [], 0
+    for n in (512, 512, 256, 128):
+        if width - lo >= n:
+            out.append((lo, n))
+            lo = lo + n
+    return out
 
 
 def tile_list_tabgate_bias_kernel(tc, tab_words, tab_scales, w4_words, w4_scales, c, u, gT, b, offs, out):
@@ -32,156 +41,125 @@ def tile_list_tabgate_bias_kernel(tc, tab_words, tab_scales, w4_words, w4_scales
         psum = ctx.enter_context(tc.psum_pool(name="psum", bufs=1))
 
         offsets = keep.tile([P, S // PER_COL], U16, name="offsets")
-        tab_plane = keep.tile([P, T // 4], I32, name="tab_plane", align_bytes=64)
+        tab_rows = keep.tile([P, T // 4], I32, name="tab_rows", align_bytes=64)
+        picked_plane = keep.tile([P, S // 4], I32, name="picked_plane", align_bytes=64)
         w4_plane = keep.tile([P, M // 4], I32, name="w4_plane", align_bytes=64)
         tab_codes = keep.tile([P, T], I32, name="tab_codes", align_bytes=64)
         w4_codes = keep.tile([P, M // 2], I32, name="w4_codes", align_bytes=64)
         u_raw = keep.tile([P, PACK, M], F32, name="u_raw")
         bias = keep.tile([P, 1], F32, name="bias")
         gates = keep.tile([P, T], F32, name="gates")
-        starts = [sum(ch[0] for ch in CHUNKS[:i]) for i in range(len(CHUNKS))]
-        c_raw = [keep.tile([P, PACK, ch[0]], F32, name="c_raw%d" % i) for i, ch in enumerate(CHUNKS)]
+        starts = [sum(ch[0] for ch in CHUNKS[:i]) for i in range(len(CHUNKS) + 1)]
+        c_raw = [keep.tile([P, PACK, ch[0]], F32, name="c_raw%d" % i, tag="shared%d" % i) for i, ch in enumerate(CHUNKS)]
         c_rows = c.rearrange("(p t) j -> p t j", t=PACK)
+        picked_rows = keep.tile([P, S], U8, name="picked_rows", align_bytes=64)
+        picked_codes = keep.tile([P, S], U32, name="picked_codes", align_bytes=64)
+        picked_gates = keep.tile([P, S], F32, name="picked_gates")
 
         def load_c(i):
-            nc.sync.dma_start(out=c_raw[i][:], in_=c_rows[:, :, starts[i] : starts[i] + CHUNKS[i][0]])
+            nc.sync.dma_start(out=c_raw[i][:], in_=c_rows[:, :, starts[i] : starts[i + 1]])
 
-        def load_plane(queue, plane, scale_rows):
-            rows = scale_rows[0].bitcast(I32)
-            for r in range(4):
-                queue.dma_start(out=plane[r:P:32, :], in_=rows[r:16:4, :])
-
-        nc.vector.memset(tab_plane[:], 0)
         nc.vector.memset(w4_plane[:], 0)
+        nc.vector.memset(tab_rows[0:112, :], 0)
+        nc.vector.memset(picked_plane[:], 0)
 
-        def ld_offs():
-            nc.sync.dma_start(offsets[:], offs)
-
-        def ld_u():
-            nc.sync.dma_start(out=u_raw[:], in_=u.rearrange("(p t) n -> p t n", t=PACK))
-
-        def ld_w4(lo, hi):
-            nc.sync.dma_start(out=w4_codes[lo:hi, :], in_=w4_words[0].bitcast(I32)[lo:hi, :])
-
-        def ld_b(queue):
-            with nc.allow_non_contiguous_dma(reason="one bias value a partition"):
-                queue.dma_start(out=bias[:], in_=b.rearrange("(p o) -> p o", o=1))
-
-        def ld_words():
-            nc.sync.dma_start(out=tab_codes[:], in_=tab_words[0].rearrange("p t i -> p (t i)").bitcast(I32))
-
-        def ld_gates():
-            nc.sync.dma_start(out=gates[:], in_=gT)
-
-        ld_offs()
-        ld_u()
-        ld_w4(0, 96)
-        load_plane(nc.sync, tab_plane, tab_scales)
-        ld_words()
-        ld_gates()
-        ld_w4(96, 128)
-        load_plane(nc.sync, w4_plane, w4_scales)
-        ld_b(nc.sync)
-        for i in range(len(CHUNKS)):
+        nc.sync.dma_start(out=tab_rows[112:P, :], in_=tab_scales[0].bitcast(I32))
+        nc.sync.dma_start(offsets[:], offs)
+        nc.sync.dma_start(out=tab_codes[:], in_=tab_words[0].rearrange("p t i -> p (t i)").bitcast(I32))
+        nc.sync.dma_start(out=u_raw[:], in_=u.rearrange("(p t) n -> p t n", t=PACK))
+        nc.sync.dma_start(out=w4_codes[:], in_=w4_words[0].bitcast(I32))
+        w4_rows = w4_scales[0].bitcast(I32)
+        for r in range(4):
+            nc.sync.dma_start(out=w4_plane[r:P:32, :], in_=w4_rows[r:16:4, :])
+        for i in range(EARLY):
             load_c(i)
+        nc.sync.dma_start(out=gates[:], in_=gT)
+        with nc.allow_non_contiguous_dma(reason="one bias value a partition"):
+            nc.sync.dma_start(out=bias[:], in_=b.rearrange("(p o) -> p o", o=1))
 
-        def cast(engine_copy, grouped, raw, lo, hi):
+        nc.vector.tensor_copy(picked_rows[:], tab_rows[:].bitcast(U8).indirect(offsets[:]))
+        for r in range(4):
+            nc.sync.dma_start(out=picked_plane[r:P:32, :], in_=picked_rows[112 + r : P : 4, :].bitcast(I32))
+        for i in range(EARLY, len(CHUNKS)):
+            load_c(i)
+        nc.vector.tensor_copy(picked_codes[:], tab_codes[:].bitcast(U32).indirect(offsets[:]))
+
+        def cast(engine_copy, grouped, raw, lo, hi, at):
             engine_copy(
-                out=grouped[:, lo:hi, :].rearrange("p (a i) t -> p a t i", i=4),
+                out=grouped[:, at + lo : at + hi, :].rearrange("p (a i) t -> p a t i", i=4),
                 in_=raw[:, :, lo:hi].rearrange("p t (a i) -> p a t i", i=4),
             )
 
-        def quantise(codes, plane, grouped, lo, hi, at):
+        codes = keep.tile([P, M + S], U32, name="codes", align_bytes=64)
+        plane = keep.tile([P, M + S], U8, name="plane", align_bytes=64)
+
+        def quantise(grouped, lo, n, at):
             nc.vector.quantize_mx(
-                out=codes[:, at + lo : at + hi].bitcast(FP8X4),
-                scales=plane[:, at + lo : at + hi],
-                in_=grouped[:, lo:hi, :].rearrange("p j t -> p (j t)"),
+                out=codes[:, at : at + n].bitcast(FP8X4),
+                scales=plane[:, at : at + n],
+                in_=grouped[:, lo : lo + n, :].rearrange("p j t -> p (j t)"),
             )
 
-        picked_plane = keep.tile([P, S], U8, name="picked_plane", align_bytes=64)
-        picked_codes = keep.tile([P, S], U32, name="picked_codes", align_bytes=64)
-        nc.vector.tensor_copy(picked_plane[:], tab_plane[:].bitcast(U8).indirect(offsets[:]))
-        nc.vector.tensor_copy(picked_codes[:], tab_codes[:].bitcast(U32).indirect(offsets[:]))
-
         u_grouped = keep.tile([P, M, PACK], BF16, name="u_grouped", align_bytes=64)
-        u_codes = keep.tile([P, M], U32, name="u_codes", align_bytes=64)
-        u_plane = keep.tile([P, M], U8, name="u_plane", align_bytes=64)
-        cast(nc.scalar.copy, u_grouped, u_raw, 0, M)
-        quantise(u_codes, u_plane, u_grouped, 0, M, 0)
+        cast(nc.scalar.copy, u_grouped, u_raw, 0, M, 0)
+        quantise(u_grouped, 0, M, 0)
 
-        c_codes = keep.tile([P, S], U32, name="c_codes", align_bytes=64)
-        c_plane = keep.tile([P, S], U8, name="c_plane", align_bytes=64)
-        picked_gates = keep.tile([P, S], F32, name="picked_gates")
-        banks = {}
-
-        def table_passes(i):
-            width, n = CHUNKS[i][0], CHUNKS[i][2]
-            for lo in range(starts[i], starts[i] + width, n):
-                banks[lo] = psum.tile([P, n], F32, name="bank%d" % lo)
+        banks = []
+        group_of = {}
+        for g, members in enumerate(GROUPS):
+            lo, hi = starts[members[0]], starts[members[-1] + 1]
+            banks.append(psum.tile([P, hi - lo], F32, name="bank%d" % g))
+            for i in members:
+                group_of[i] = g
+            n = 512 if hi - lo == 512 else 128
+            for at in range(lo, hi, n):
                 nc.tensor.matmul_mx(
-                    out=banks[lo][:],
+                    out=banks[g][:, at - lo : at - lo + n],
                     lhsT=w4_codes[:].bitcast(FP4X4),
                     lhsT_scale=w4_plane[:].bitcast(U8),
-                    rhs=picked_codes[:, lo : lo + n].bitcast(FP8X4),
-                    rhs_scale=picked_plane[:, lo : lo + n],
-                    start=True,
+                    rhs=picked_codes[:, at : at + n].bitcast(FP8X4),
+                    rhs_scale=picked_plane[:].bitcast(U8)[:, at : at + n],
+                    start=(at == lo),
                     stop=False,
                 )
 
-        summed = {}
-
         def front(i):
-            width, on_vector, n, q, fused = CHUNKS[i]
-            at = starts[i]
-            grouped = keep.tile([P, width, PACK], BF16, name="grouped%d" % i, align_bytes=64)
-            if on_vector > 0:
-                cast(nc.vector.tensor_copy, grouped, c_raw[i], 0, on_vector)
+            width, on_vector = CHUNKS[i]
+            lead = 0
+            grouped = keep.tile([P, lead + width, PACK], BF16, name="grouped%d" % i, align_bytes=64)
             if on_vector < width:
-                cast(nc.scalar.copy, grouped, c_raw[i], on_vector, width)
-            for lo in range(0, width, q):
-                quantise(c_codes, c_plane, grouped, lo, lo + q, at)
-            for lo in range(at, at + width, n):
+                cast(nc.scalar.copy, grouped, c_raw[i], on_vector, width, lead)
+            if on_vector > 0:
+                cast(nc.vector.tensor_copy, grouped, c_raw[i], 0, on_vector, lead)
+            for lo, n in pieces(lead + width):
+                quantise(grouped, lo, n, M + starts[i] - lead + lo)
+            g = group_of[i]
+            base = starts[GROUPS[g][0]]
+            cut = pieces(width)
+            for lo, n in cut:
+                at = starts[i] + lo
                 nc.tensor.matmul_mx(
-                    out=banks[lo][:],
-                    lhsT=u_codes[:].bitcast(FP8X4),
-                    lhsT_scale=u_plane[:],
-                    rhs=c_codes[:, lo : lo + n].bitcast(FP8X4),
-                    rhs_scale=c_plane[:, lo : lo + n],
+                    out=banks[g][:, at - base : at - base + n],
+                    lhsT=codes[:, 0:M].bitcast(FP8X4),
+                    lhsT_scale=plane[:, 0:M],
+                    rhs=codes[:, M + at : M + at + n].bitcast(FP8X4),
+                    rhs_scale=plane[:, M + at : M + at + n],
                     start=False,
-                    stop=True,
+                    stop=(i == GROUPS[g][-1] and lo == cut[-1][0]),
                 )
-            if fused:
-                summed[i] = keep.tile([P, width], F32, name="summed%d" % i)
-                for lo in range(at, at + width, n):
-                    nc.scalar.activation(out=summed[i][:, lo - at : lo - at + n], in_=banks[lo][:], func=IDENTITY, bias=bias[:])
 
-        def back(i):
-            width, on_vector, n, q, fused = CHUNKS[i]
-            at = starts[i]
-            result = keep.tile([P, width], F32, name="result%d" % i)
-            if fused:
-                window = gates[:].indirect(offsets[:, at // PER_COL : (at + width) // PER_COL])
-                nc.vector.tensor_tensor(result[:], window, summed[i][:], MULT)
-            else:
-                for lo in range(at, at + width, n):
-                    nc.vector.scalar_tensor_tensor(
-                        out=result[:, lo - at : lo - at + n],
-                        in0=banks[lo][:],
-                        scalar=bias[:],
-                        in1=picked_gates[:, lo : lo + n],
-                        op0=ADD,
-                        op1=MULT,
-                    )
-            nc.sync.dma_start(out=out[:, at : at + width], in_=result[:])
-
-        def pick_gates(lo):
-            window = gates[:].indirect(offsets[:, lo // PER_COL : (lo + GATE_PIECE) // PER_COL])
-            nc.vector.tensor_copy(picked_gates[:, lo : lo + GATE_PIECE], window)
+        def back(g):
+            lo, hi = starts[GROUPS[g][0]], starts[GROUPS[g][-1] + 1]
+            result = keep.tile([P, hi - lo], F32, name="result%d" % g, tag="shared%d" % (GROUPS[g][-1] + 1))
+            nc.vector.scalar_tensor_tensor(
+                out=result[:], in0=banks[g][:], scalar=bias[:], in1=picked_gates[:, lo:hi], op0=ADD, op1=MULT
+            )
+            nc.sync.dma_start(out=out[:, lo:hi], in_=result[:])
 
         for i in range(len(CHUNKS)):
-            table_passes(i)
-        pick_gates(0)
-        for i in range(len(CHUNKS)):
+            if i == EARLY:
+                nc.vector.tensor_copy(picked_gates[:], gates[:].indirect(offsets[:]))
             front(i)
-        for i in range(len(CHUNKS)):
-            back(i)
+            if i > 0 and group_of[i - 1] != group_of[i]:
+                back(group_of[i - 1])
+        back(len(GROUPS) - 1)

@@ -20,9 +20,9 @@ P = 128
 PACK = 4
 PER_COL = 16
 
-CHUNKS = [(256, 0), (256, 0), (256, 0), (256, 128), (256, 0), (256, 128), (256, 0), (128, 0), (128, 0)]
+CHUNKS = [(512, 192), (512, 320), (256, 0), (256, 0), (256, 128), (128, 0), (128, 0)]
 EARLY = 0
-GROUPS = [[0, 1], [2, 3], [4], [5], [6], [7], [8]]
+GROUPS = [[0], [1], [2], [3], [4], [5], [6]]
 
 
 def pieces(width):

@@ -129,7 +129,16 @@ def tile_list_tabgate_bias_kernel(tc, tab_words, tab_scales, w4_words, w4_scales
             grouped = keep.tile([P, lead + width, PACK], BF16, name="grouped%d" % i, align_bytes=64)
             if on_vector < width:
                 cast(nc.scalar.copy, grouped, c_raw[i], on_vector, width, lead)
-            if on_vector > 0:
+            if i == 0:
+                nc.gpsimd.tensor_scalar(
+                    out=grouped[:, 0:on_vector, :],
+                    in0=c_raw[i][:, :, 0:on_vector].rearrange("p t j -> p j t"),
+                    scalar1=1.0,
+                    scalar2=0.0,
+                    op0=MULT,
+                    op1=ADD,
+                )
+            elif on_vector > 0:
                 cast(nc.vector.tensor_copy, grouped, c_raw[i], 0, on_vector, lead)
             for lo, n in pieces(lead + width):
                 quantise(grouped, lo, n, M + starts[i] - lead + lo)

@@ -20,14 +20,15 @@ P = 128
 PACK = 4
 PER_COL = 16
 
-CHUNKS = [(512, 192), (512, 320), (256, 0), (256, 0), (256, 128), (128, 0), (128, 0)]
-EARLY = 0
+CHUNKS = [(512, 0), (512, 320), (256, 0), (256, 0), (256, 160), (128, 0), (128, 0)]
+ON_GPSIMD = 192
 GROUPS = [[0], [1], [2], [3], [4], [5], [6]]
+HELD_BY = {0: 1, 1: 2, 2: 3, 3: 4, 4: 6}
 
 
 def pieces(width):
     out, lo = [], 0
-    for n in (512, 512, 256, 128):
+    for n in (512, 256, 128):
         if width - lo >= n:
             out.append((lo, n))
             lo = lo + n
@@ -71,8 +72,6 @@ def tile_list_tabgate_bias_kernel(tc, tab_words, tab_scales, w4_words, w4_scales
         w4_rows = w4_scales[0].bitcast(I32)
         for r in range(4):
             nc.sync.dma_start(out=w4_plane[r:P:32, :], in_=w4_rows[r:16:4, :])
-        for i in range(EARLY):
-            load_c(i)
         nc.sync.dma_start(out=gates[:], in_=gT)
         with nc.allow_non_contiguous_dma(reason="one bias value a partition"):
             nc.sync.dma_start(out=bias[:], in_=b.rearrange("(p o) -> p o", o=1))
@@ -80,14 +79,14 @@ def tile_list_tabgate_bias_kernel(tc, tab_words, tab_scales, w4_words, w4_scales
         nc.vector.tensor_copy(picked_rows[:], tab_rows[:].bitcast(U8).indirect(offsets[:]))
         for r in range(4):
             nc.sync.dma_start(out=picked_plane[r:P:32, :], in_=picked_rows[112 + r : P : 4, :].bitcast(I32))
-        for i in range(EARLY, len(CHUNKS)):
+        for i in range(len(CHUNKS)):
             load_c(i)
         nc.vector.tensor_copy(picked_codes[:], tab_codes[:].bitcast(U32).indirect(offsets[:]))
 
         def cast(engine_copy, grouped, raw, lo, hi, at):
             engine_copy(
-                out=grouped[:, at + lo : at + hi, :].rearrange("p (a i) t -> p a t i", i=4),
-                in_=raw[:, :, lo:hi].rearrange("p t (a i) -> p a t i", i=4),
+                out=grouped[:, at + lo : at + hi, :].rearrange("p (a i) t -> p a t i", i=2),
+                in_=raw[:, :, lo:hi].rearrange("p t (a i) -> p a t i", i=2),
             )
 
         codes = keep.tile([P, M + S], U32, name="codes", align_bytes=64)
@@ -123,28 +122,31 @@ def tile_list_tabgate_bias_kernel(tc, tab_words, tab_scales, w4_words, w4_scales
                     stop=False,
                 )
 
-        def front(i):
+        grouped = [keep.tile([P, ch[0], PACK], BF16, name="grouped%d" % i, align_bytes=64) for i, ch in enumerate(CHUNKS)]
+
+        def round_chunk(i):
             width, on_vector = CHUNKS[i]
-            lead = 0
-            grouped = keep.tile([P, lead + width, PACK], BF16, name="grouped%d" % i, align_bytes=64)
-            if on_vector < width:
-                cast(nc.scalar.copy, grouped, c_raw[i], on_vector, width, lead)
+            first = ON_GPSIMD if i == 0 else on_vector
+            cast(nc.scalar.copy, grouped[i], c_raw[i], first, width, 0)
             if i == 0:
                 nc.gpsimd.tensor_scalar(
-                    out=grouped[:, 0:on_vector, :],
-                    in0=c_raw[i][:, :, 0:on_vector].rearrange("p t j -> p j t"),
+                    out=grouped[i][:, 0:first, :],
+                    in0=c_raw[i][:, :, 0:first].rearrange("p t j -> p j t"),
                     scalar1=1.0,
                     scalar2=0.0,
                     op0=MULT,
                     op1=ADD,
                 )
             elif on_vector > 0:
-                cast(nc.vector.tensor_copy, grouped, c_raw[i], 0, on_vector, lead)
-            for lo, n in pieces(lead + width):
-                quantise(grouped, lo, n, M + starts[i] - lead + lo)
+                cast(nc.vector.tensor_copy, grouped[i], c_raw[i], 0, on_vector, 0)
+
+        def multiply(i):
+            width = CHUNKS[i][0]
             g = group_of[i]
             base = starts[GROUPS[g][0]]
             cut = pieces(width)
+            for lo, n in cut:
+                quantise(grouped[i], lo, n, M + starts[i] + lo)
             for lo, n in cut:
                 at = starts[i] + lo
                 nc.tensor.matmul_mx(
@@ -157,18 +159,42 @@ def tile_list_tabgate_bias_kernel(tc, tab_words, tab_scales, w4_words, w4_scales
                     stop=(i == GROUPS[g][-1] and lo == cut[-1][0]),
                 )
 
-        def back(g):
-            lo, hi = starts[GROUPS[g][0]], starts[GROUPS[g][-1] + 1]
-            result = keep.tile([P, hi - lo], F32, name="result%d" % g, tag="shared%d" % (GROUPS[g][-1] + 1))
-            nc.vector.scalar_tensor_tensor(
-                out=result[:], in0=banks[g][:], scalar=bias[:], in1=picked_gates[:, lo:hi], op0=ADD, op1=MULT
-            )
-            nc.sync.dma_start(out=out[:, lo:hi], in_=result[:])
+        results = {}
 
-        for i in range(len(CHUNKS)):
-            if i == EARLY:
-                nc.vector.tensor_copy(picked_gates[:], gates[:].indirect(offsets[:]))
-            front(i)
-            if i > 0 and group_of[i - 1] != group_of[i]:
-                back(group_of[i - 1])
-        back(len(GROUPS) - 1)
+        def finish(g):
+            lo, hi = starts[GROUPS[g][0]], starts[GROUPS[g][-1] + 1]
+            if g == 5:
+                result = results[4][:, CHUNKS[4][0] :]
+            else:
+                tag = "shared%d" % HELD_BY[g] if g in HELD_BY else "result%d" % g
+                room = hi - lo + (CHUNKS[5][0] if g == 4 else 0)
+                tile = keep.tile([P, room], F32, name="result%d" % g, tag=tag)
+                results.setdefault(g, tile)
+                result = tile[:, 0 : hi - lo]
+            nc.vector.scalar_tensor_tensor(
+                out=result, in0=banks[g][:], scalar=bias[:], in1=picked_gates[:, lo:hi], op0=ADD, op1=MULT
+            )
+            nc.sync.dma_start(out=out[:, lo:hi], in_=result)
+
+        nc.vector.tensor_copy(picked_gates[:], gates[:].indirect(offsets[:]))
+        round_chunk(0)
+        multiply(0)
+        round_chunk(1)
+        multiply(1)
+        finish(0)
+        round_chunk(2)
+        multiply(2)
+        finish(1)
+        round_chunk(3)
+        multiply(3)
+        round_chunk(4)
+        finish(2)
+        multiply(4)
+        finish(3)
+        round_chunk(5)
+        multiply(5)
+        round_chunk(6)
+        multiply(6)
+        finish(4)
+        finish(5)
+        finish(6)

@@ -19,24 +19,18 @@ MULT = mybir.AluOpType.mult
 P = 128
 PACK = 4
 PER_COL = 16
+SCALE_ROWS = K // 32
+STAGED = P - SCALE_ROWS
+QUADRANT = 32
 
-CHUNKS = [(512, 0), (512, 320), (256, 0), (256, 0), (256, 160), (128, 0), (128, 0)]
-ON_GPSIMD = 192
-GROUPS = [[0], [1], [2], [3], [4], [5], [6]]
-HELD_BY = {0: 1, 1: 2, 2: 3, 3: 4, 4: 6}
-
-
-def pieces(width):
-    out, lo = [], 0
-    for n in (512, 256, 128):
-        if width - lo >= n:
-            out.append((lo, n))
-            lo = lo + n
-    return out
+WIDTHS = [512] * 2 + [256] * 3 + [128] * 2
+ON_VECTOR = {1: 320, 4: 128}
 
 
 def tile_list_tabgate_bias_kernel(tc, tab_words, tab_scales, w4_words, w4_scales, c, u, gT, b, offs, out):
     nc = tc.nc
+    chunks = range(len(WIDTHS))
+    starts = [sum(WIDTHS[:i]) for i in range(len(WIDTHS) + 1)]
     with ExitStack() as ctx:
         keep = ctx.enter_context(tc.tile_pool(name="keep", bufs=1))
         psum = ctx.enter_context(tc.psum_pool(name="psum", bufs=1))
@@ -50,151 +44,107 @@ def tile_list_tabgate_bias_kernel(tc, tab_words, tab_scales, w4_words, w4_scales
         u_raw = keep.tile([P, PACK, M], F32, name="u_raw")
         bias = keep.tile([P, 1], F32, name="bias")
         gates = keep.tile([P, T], F32, name="gates")
-        starts = [sum(ch[0] for ch in CHUNKS[:i]) for i in range(len(CHUNKS) + 1)]
-        c_raw = [keep.tile([P, PACK, ch[0]], F32, name="c_raw%d" % i, tag="shared%d" % i) for i, ch in enumerate(CHUNKS)]
-        c_rows = c.rearrange("(p t) j -> p t j", t=PACK)
+        c_raw = [keep.tile([P, PACK, WIDTHS[i]], F32, name="c_raw%d" % i, tag="shared%d" % i) for i in chunks]
         picked_rows = keep.tile([P, S], U8, name="picked_rows", align_bytes=64)
         picked_codes = keep.tile([P, S], U32, name="picked_codes", align_bytes=64)
         picked_gates = keep.tile([P, S], F32, name="picked_gates")
 
-        def load_c(i):
-            nc.sync.dma_start(out=c_raw[i][:], in_=c_rows[:, :, starts[i] : starts[i + 1]])
-
         nc.vector.memset(w4_plane[:], 0)
-        nc.vector.memset(tab_rows[0:112, :], 0)
+        nc.vector.memset(tab_rows[0:STAGED, :], 0)
         nc.vector.memset(picked_plane[:], 0)
 
-        nc.sync.dma_start(out=tab_rows[112:P, :], in_=tab_scales[0].bitcast(I32))
+        nc.sync.dma_start(out=tab_rows[STAGED:P, :], in_=tab_scales[0].bitcast(I32))
         nc.sync.dma_start(offsets[:], offs)
         nc.sync.dma_start(out=tab_codes[:], in_=tab_words[0].rearrange("p t i -> p (t i)").bitcast(I32))
         nc.sync.dma_start(out=u_raw[:], in_=u.rearrange("(p t) n -> p t n", t=PACK))
         nc.sync.dma_start(out=w4_codes[:], in_=w4_words[0].bitcast(I32))
         w4_rows = w4_scales[0].bitcast(I32)
         for r in range(4):
-            nc.sync.dma_start(out=w4_plane[r:P:32, :], in_=w4_rows[r:16:4, :])
+            nc.sync.dma_start(out=w4_plane[r:P:QUADRANT, :], in_=w4_rows[r:SCALE_ROWS:4, :])
         nc.sync.dma_start(out=gates[:], in_=gT)
         with nc.allow_non_contiguous_dma(reason="one bias value a partition"):
             nc.sync.dma_start(out=bias[:], in_=b.rearrange("(p o) -> p o", o=1))
 
         nc.vector.tensor_copy(picked_rows[:], tab_rows[:].bitcast(U8).indirect(offsets[:]))
         for r in range(4):
-            nc.sync.dma_start(out=picked_plane[r:P:32, :], in_=picked_rows[112 + r : P : 4, :].bitcast(I32))
-        for i in range(len(CHUNKS)):
-            load_c(i)
+            nc.sync.dma_start(out=picked_plane[r:P:QUADRANT, :], in_=picked_rows[STAGED + r : P : 4, :].bitcast(I32))
+        c_rows = c.rearrange("(p t) j -> p t j", t=PACK)
+        for i in chunks:
+            nc.sync.dma_start(out=c_raw[i][:], in_=c_rows[:, :, starts[i] : starts[i + 1]])
         nc.vector.tensor_copy(picked_codes[:], tab_codes[:].bitcast(U32).indirect(offsets[:]))
 
-        def cast(engine_copy, grouped, raw, lo, hi, at):
+        def round_columns(engine_copy, grouped, raw, lo, hi):
             engine_copy(
-                out=grouped[:, at + lo : at + hi, :].rearrange("p (a i) t -> p a t i", i=2),
+                out=grouped[:, lo:hi, :].rearrange("p (a i) t -> p a t i", i=2),
                 in_=raw[:, :, lo:hi].rearrange("p t (a i) -> p a t i", i=2),
             )
 
         codes = keep.tile([P, M + S], U32, name="codes", align_bytes=64)
         plane = keep.tile([P, M + S], U8, name="plane", align_bytes=64)
 
-        def quantise(grouped, lo, n, at):
+        def quantise(grouped, lo, hi):
             nc.vector.quantize_mx(
-                out=codes[:, at : at + n].bitcast(FP8X4),
-                scales=plane[:, at : at + n],
-                in_=grouped[:, lo : lo + n, :].rearrange("p j t -> p (j t)"),
+                out=codes[:, lo:hi].bitcast(FP8X4),
+                scales=plane[:, lo:hi],
+                in_=grouped[:].rearrange("p j t -> p (j t)"),
             )
 
         u_grouped = keep.tile([P, M, PACK], BF16, name="u_grouped", align_bytes=64)
-        cast(nc.scalar.copy, u_grouped, u_raw, 0, M, 0)
-        quantise(u_grouped, 0, M, 0)
+        round_columns(nc.scalar.copy, u_grouped, u_raw, 0, M)
+        quantise(u_grouped, 0, M)
 
-        banks = []
-        group_of = {}
-        for g, members in enumerate(GROUPS):
-            lo, hi = starts[members[0]], starts[members[-1] + 1]
-            banks.append(psum.tile([P, hi - lo], F32, name="bank%d" % g))
-            for i in members:
-                group_of[i] = g
-            n = 512 if hi - lo == 512 else 128
-            for at in range(lo, hi, n):
+        banks = [psum.tile([P, WIDTHS[i]], F32, name="bank%d" % i) for i in chunks]
+        for i in chunks:
+            n = 512 if WIDTHS[i] == 512 else 128
+            for at in range(0, WIDTHS[i], n):
+                cols = slice(starts[i] + at, starts[i] + at + n)
                 nc.tensor.matmul_mx(
-                    out=banks[g][:, at - lo : at - lo + n],
+                    out=banks[i][:, at : at + n],
                     lhsT=w4_codes[:].bitcast(FP4X4),
                     lhsT_scale=w4_plane[:].bitcast(U8),
-                    rhs=picked_codes[:, at : at + n].bitcast(FP8X4),
-                    rhs_scale=picked_plane[:].bitcast(U8)[:, at : at + n],
-                    start=(at == lo),
+                    rhs=picked_codes[:, cols].bitcast(FP8X4),
+                    rhs_scale=picked_plane[:].bitcast(U8)[:, cols],
+                    start=(at == 0),
                     stop=False,
                 )
 
-        grouped = [keep.tile([P, ch[0], PACK], BF16, name="grouped%d" % i, align_bytes=64) for i, ch in enumerate(CHUNKS)]
+        grouped = [keep.tile([P, WIDTHS[i], PACK], BF16, name="grouped%d" % i, align_bytes=64) for i in chunks]
 
         def round_chunk(i):
-            width, on_vector = CHUNKS[i]
-            first = ON_GPSIMD if i == 0 else on_vector
-            cast(nc.scalar.copy, grouped[i], c_raw[i], first, width, 0)
-            if i == 0:
-                nc.gpsimd.tensor_scalar(
-                    out=grouped[i][:, 0:first, :],
-                    in0=c_raw[i][:, :, 0:first].rearrange("p t j -> p j t"),
-                    scalar1=1.0,
-                    scalar2=0.0,
-                    op0=MULT,
-                    op1=ADD,
-                )
-            elif on_vector > 0:
-                cast(nc.vector.tensor_copy, grouped[i], c_raw[i], 0, on_vector, 0)
+            on_vector = ON_VECTOR.get(i, 0)
+            round_columns(nc.scalar.copy, grouped[i], c_raw[i], on_vector, WIDTHS[i])
+            if on_vector > 0:
+                round_columns(nc.vector.tensor_copy, grouped[i], c_raw[i], 0, on_vector)
 
         def multiply(i):
-            width = CHUNKS[i][0]
-            g = group_of[i]
-            base = starts[GROUPS[g][0]]
-            cut = pieces(width)
-            for lo, n in cut:
-                quantise(grouped[i], lo, n, M + starts[i] + lo)
-            for lo, n in cut:
-                at = starts[i] + lo
-                nc.tensor.matmul_mx(
-                    out=banks[g][:, at - base : at - base + n],
-                    lhsT=codes[:, 0:M].bitcast(FP8X4),
-                    lhsT_scale=plane[:, 0:M],
-                    rhs=codes[:, M + at : M + at + n].bitcast(FP8X4),
-                    rhs_scale=plane[:, M + at : M + at + n],
-                    start=False,
-                    stop=(i == GROUPS[g][-1] and lo == cut[-1][0]),
-                )
-
-        results = {}
-
-        def finish(g):
-            lo, hi = starts[GROUPS[g][0]], starts[GROUPS[g][-1] + 1]
-            if g == 5:
-                result = results[4][:, CHUNKS[4][0] :]
-            else:
-                tag = "shared%d" % HELD_BY[g] if g in HELD_BY else "result%d" % g
-                room = hi - lo + (CHUNKS[5][0] if g == 4 else 0)
-                tile = keep.tile([P, room], F32, name="result%d" % g, tag=tag)
-                results.setdefault(g, tile)
-                result = tile[:, 0 : hi - lo]
-            nc.vector.scalar_tensor_tensor(
-                out=result, in0=banks[g][:], scalar=bias[:], in1=picked_gates[:, lo:hi], op0=ADD, op1=MULT
+            lo, hi = M + starts[i], M + starts[i + 1]
+            quantise(grouped[i], lo, hi)
+            nc.tensor.matmul_mx(
+                out=banks[i][:],
+                lhsT=codes[:, 0:M].bitcast(FP8X4),
+                lhsT_scale=plane[:, 0:M],
+                rhs=codes[:, lo:hi].bitcast(FP8X4),
+                rhs_scale=plane[:, lo:hi],
+                start=False,
+                stop=True,
             )
-            nc.sync.dma_start(out=out[:, lo:hi], in_=result)
+
+        def finish(i):
+            tag = "shared%d" % (i + 1)
+            result = keep.tile([P, WIDTHS[i]], F32, name="result%d" % i, tag=tag)
+            cols = slice(starts[i], starts[i + 1])
+            nc.vector.scalar_tensor_tensor(
+                out=result[:], in0=banks[i][:], scalar=bias[:], in1=picked_gates[:, cols], op0=ADD, op1=MULT
+            )
+            nc.sync.dma_start(out=out[:, cols], in_=result[:])
 
         nc.vector.tensor_copy(picked_gates[:], gates[:].indirect(offsets[:]))
+
         round_chunk(0)
-        multiply(0)
-        round_chunk(1)
-        multiply(1)
-        finish(0)
-        round_chunk(2)
-        multiply(2)
-        finish(1)
-        round_chunk(3)
-        multiply(3)
-        round_chunk(4)
-        finish(2)
-        multiply(4)
-        finish(3)
-        round_chunk(5)
-        multiply(5)
-        round_chunk(6)
-        multiply(6)
-        finish(4)
-        finish(5)
-        finish(6)
+        for i in chunks:
+            if i + 1 < len(WIDTHS):
+                round_chunk(i + 1)
+            multiply(i)
+            if i > 0:
+                finish(i - 1)
+        finish(len(WIDTHS) - 1)

@@ -23,8 +23,8 @@ SCALE_ROWS = K // 32
 STAGED = P - SCALE_ROWS
 QUADRANT = 32
 
-WIDTHS = [512] * 2 + [256] * 3 + [128] * 2
-ON_VECTOR = {1: 320, 4: 128}
+WIDTHS = [256] + [512] * 2 + [256] * 2 + [128] * 2
+ON_VECTOR = {1: 160, 2: 256, 4: 96, 6: 64}
 
 
 def tile_list_tabgate_bias_kernel(tc, tab_words, tab_scales, w4_words, w4_scales, c, u, gT, b, offs, out):
@@ -129,22 +129,29 @@ def tile_list_tabgate_bias_kernel(tc, tab_words, tab_scales, w4_words, w4_scales
                 stop=True,
             )
 
-        def finish(i):
-            tag = "shared%d" % (i + 1)
-            result = keep.tile([P, WIDTHS[i]], F32, name="result%d" % i, tag=tag)
+        def finish(i, result):
             cols = slice(starts[i], starts[i + 1])
             nc.vector.scalar_tensor_tensor(
-                out=result[:], in0=banks[i][:], scalar=bias[:], in1=picked_gates[:, cols], op0=ADD, op1=MULT
+                out=result, in0=banks[i][:], scalar=bias[:], in1=picked_gates[:, cols], op0=ADD, op1=MULT
             )
-            nc.sync.dma_start(out=out[:, cols], in_=result[:])
+            nc.sync.dma_start(out=out[:, cols], in_=result)
+
+        def result_tile(width, held_by):
+            return keep.tile([P, width], F32, name="result%d" % held_by, tag="shared%d" % held_by)
 
         nc.vector.tensor_copy(picked_gates[:], gates[:].indirect(offsets[:]))
 
+        last = len(WIDTHS) - 1
         round_chunk(0)
-        for i in chunks:
-            if i + 1 < len(WIDTHS):
-                round_chunk(i + 1)
+        for i in range(last - 1):
+            round_chunk(i + 1)
             multiply(i)
             if i > 0:
-                finish(i - 1)
-        finish(len(WIDTHS) - 1)
+                finish(i - 1, result_tile(WIDTHS[i - 1], i)[:])
+        round_chunk(last)
+        multiply(last - 1)
+        multiply(last)
+        held = result_tile(WIDTHS[last - 2] + WIDTHS[last - 1], last)
+        finish(last - 2, held[:, 0 : WIDTHS[last - 2]])
+        finish(last - 1, held[:, WIDTHS[last - 2] :])
+        finish(last, result_tile(WIDTHS[last], last + 1)[:])

@@ -20,7 +20,7 @@ P = 128
 PACK = 4
 PER_COL = 16
 SCALE_ROWS = K // 32
-STAGED = P - SCALE_ROWS
+STAGE_FROM, STAGE_STEP = 32, 4
 QUADRANT = 32
 
 WIDTHS = [256] + [512] * 2 + [256] * 2 + [128] * 2
@@ -49,25 +49,28 @@ def tile_list_tabgate_bias_kernel(tc, tab_words, tab_scales, w4_words, w4_scales
         picked_codes = keep.tile([P, S], U32, name="picked_codes", align_bytes=64)
         picked_gates = keep.tile([P, S], F32, name="picked_gates")
 
+        nc.vector.memset(tab_rows[:], 0)
         nc.vector.memset(w4_plane[:], 0)
-        nc.vector.memset(tab_rows[0:STAGED, :], 0)
         nc.vector.memset(picked_plane[:], 0)
 
-        nc.sync.dma_start(out=tab_rows[STAGED:P, :], in_=tab_scales[0].bitcast(I32))
+        staged = slice(STAGE_FROM, STAGE_FROM + STAGE_STEP * SCALE_ROWS, STAGE_STEP)
         nc.sync.dma_start(offsets[:], offs)
-        nc.sync.dma_start(out=tab_codes[:], in_=tab_words[0].rearrange("p t i -> p (t i)").bitcast(I32))
         nc.sync.dma_start(out=u_raw[:], in_=u.rearrange("(p t) n -> p t n", t=PACK))
+        with nc.allow_non_contiguous_dma(reason="one bias value a partition"):
+            nc.sync.dma_start(out=bias[:], in_=b.rearrange("(p o) -> p o", o=1))
+        nc.sync.dma_start(out=tab_rows[staged, :], in_=tab_scales[0].bitcast(I32))
+        nc.sync.dma_start(out=tab_codes[:], in_=tab_words[0].rearrange("p t i -> p (t i)").bitcast(I32))
         nc.sync.dma_start(out=w4_codes[:], in_=w4_words[0].bitcast(I32))
         w4_rows = w4_scales[0].bitcast(I32)
         for r in range(4):
             nc.sync.dma_start(out=w4_plane[r:P:QUADRANT, :], in_=w4_rows[r:SCALE_ROWS:4, :])
         nc.sync.dma_start(out=gates[:], in_=gT)
-        with nc.allow_non_contiguous_dma(reason="one bias value a partition"):
-            nc.sync.dma_start(out=bias[:], in_=b.rearrange("(p o) -> p o", o=1))
 
         nc.vector.tensor_copy(picked_rows[:], tab_rows[:].bitcast(U8).indirect(offsets[:]))
         for r in range(4):
-            nc.sync.dma_start(out=picked_plane[r:P:QUADRANT, :], in_=picked_rows[STAGED + r : P : 4, :].bitcast(I32))
+            first = STAGE_FROM + STAGE_STEP * r
+            rows = slice(first, first + STAGE_STEP * SCALE_ROWS, 4 * STAGE_STEP)
+            nc.sync.dma_start(out=picked_plane[r:P:QUADRANT, :], in_=picked_rows[rows, :].bitcast(I32))
         c_rows = c.rearrange("(p t) j -> p t j", t=PACK)
         for i in chunks:
             nc.sync.dma_start(out=c_raw[i][:], in_=c_rows[:, :, starts[i] : starts[i + 1]])

@@ -24,7 +24,10 @@ STAGE_FROM, STAGE_STEP = 32, 4
 QUADRANT = 32
 
 WIDTHS = [256] + [512] * 2 + [256] * 2 + [128] * 2
-ON_VECTOR = {1: 160, 2: 256, 4: 96, 6: 64}
+ON_VECTOR = {1: 128, 2: 192, 4: 96, 6: 64}
+FIRST = 32
+LATE = 512
+OVERLAP = 16
 
 
 def tile_list_tabgate_bias_kernel(tc, tab_words, tab_scales, w4_words, w4_scales, c, u, gT, b, offs, out):
@@ -44,27 +47,30 @@ def tile_list_tabgate_bias_kernel(tc, tab_words, tab_scales, w4_words, w4_scales
         u_raw = keep.tile([P, PACK, M], F32, name="u_raw")
         bias = keep.tile([P, 1], F32, name="bias")
         gates = keep.tile([P, T], F32, name="gates")
-        c_raw = [keep.tile([P, PACK, WIDTHS[i]], F32, name="c_raw%d" % i, tag="shared%d" % i) for i in chunks]
+        ahead = [0, LATE - OVERLAP] + [WIDTHS[i - 2] - OVERLAP for i in range(2, len(WIDTHS) - 1)] + [0]
+        landing = [keep.tile([P, ahead[i] + PACK * WIDTHS[i]], F32, name="landing%d" % i, tag="shared%d" % i) for i in chunks]
+        c_raw = [landing[i][:, ahead[i] :].rearrange("p (t j) -> p t j", t=PACK) for i in chunks]
         picked_rows = keep.tile([P, S], U8, name="picked_rows", align_bytes=64)
         picked_codes = keep.tile([P, S], U32, name="picked_codes", align_bytes=64)
-        picked_gates = keep.tile([P, S], F32, name="picked_gates")
+        picked_gates = keep.tile([P, S - LATE], F32, name="picked_gates")
 
-        nc.vector.memset(tab_rows[:], 0)
         nc.vector.memset(w4_plane[:], 0)
+        nc.vector.memset(tab_rows[:], 0)
         nc.vector.memset(picked_plane[:], 0)
 
         staged = slice(STAGE_FROM, STAGE_FROM + STAGE_STEP * SCALE_ROWS, STAGE_STEP)
         nc.sync.dma_start(offsets[:], offs)
         nc.sync.dma_start(out=u_raw[:], in_=u.rearrange("(p t) n -> p t n", t=PACK))
-        with nc.allow_non_contiguous_dma(reason="one bias value a partition"):
-            nc.sync.dma_start(out=bias[:], in_=b.rearrange("(p o) -> p o", o=1))
+        w4_rows = w4_scales[0].bitcast(I32)
+        nc.sync.dma_start(out=w4_plane[0:P:QUADRANT, :], in_=w4_rows[0:SCALE_ROWS:4, :])
         nc.sync.dma_start(out=tab_rows[staged, :], in_=tab_scales[0].bitcast(I32))
         nc.sync.dma_start(out=tab_codes[:], in_=tab_words[0].rearrange("p t i -> p (t i)").bitcast(I32))
         nc.sync.dma_start(out=w4_codes[:], in_=w4_words[0].bitcast(I32))
-        w4_rows = w4_scales[0].bitcast(I32)
-        for r in range(4):
+        for r in range(1, 4):
             nc.sync.dma_start(out=w4_plane[r:P:QUADRANT, :], in_=w4_rows[r:SCALE_ROWS:4, :])
         nc.sync.dma_start(out=gates[:], in_=gT)
+        with nc.allow_non_contiguous_dma(reason="one bias value a partition"):
+            nc.sync.dma_start(out=bias[:], in_=b.rearrange("(p o) -> p o", o=1))
 
         nc.vector.tensor_copy(picked_rows[:], tab_rows[:].bitcast(U8).indirect(offsets[:]))
         for r in range(4):
@@ -73,7 +79,7 @@ def tile_list_tabgate_bias_kernel(tc, tab_words, tab_scales, w4_words, w4_scales
             nc.sync.dma_start(out=picked_plane[r:P:QUADRANT, :], in_=picked_rows[rows, :].bitcast(I32))
         c_rows = c.rearrange("(p t) j -> p t j", t=PACK)
         for i in chunks:
-            nc.sync.dma_start(out=c_raw[i][:], in_=c_rows[:, :, starts[i] : starts[i + 1]])
+            nc.sync.dma_start(out=c_raw[i], in_=c_rows[:, :, starts[i] : starts[i + 1]])
         nc.vector.tensor_copy(picked_codes[:], tab_codes[:].bitcast(U32).indirect(offsets[:]))
 
         def round_columns(engine_copy, grouped, raw, lo, hi):
@@ -114,10 +120,13 @@ def tile_list_tabgate_bias_kernel(tc, tab_words, tab_scales, w4_words, w4_scales
         grouped = [keep.tile([P, WIDTHS[i], PACK], BF16, name="grouped%d" % i, align_bytes=64) for i in chunks]
 
         def round_chunk(i):
-            on_vector = ON_VECTOR.get(i, 0)
-            round_columns(nc.scalar.copy, grouped[i], c_raw[i], on_vector, WIDTHS[i])
-            if on_vector > 0:
-                round_columns(nc.vector.tensor_copy, grouped[i], c_raw[i], 0, on_vector)
+            on_scalar = WIDTHS[i] - ON_VECTOR.get(i, 0)
+            first = FIRST if ahead[i] > 0 else 0
+            if first > 0:
+                round_columns(nc.scalar.copy, grouped[i], c_raw[i], 0, first)
+            round_columns(nc.scalar.copy, grouped[i], c_raw[i], first, on_scalar)
+            if on_scalar < WIDTHS[i]:
+                round_columns(nc.vector.tensor_copy, grouped[i], c_raw[i], on_scalar, WIDTHS[i])
 
         def multiply(i):
             lo, hi = M + starts[i], M + starts[i + 1]
@@ -134,23 +143,28 @@ def tile_list_tabgate_bias_kernel(tc, tab_words, tab_scales, w4_words, w4_scales
 
         def finish(i, result):
             cols = slice(starts[i], starts[i + 1])
-            nc.vector.scalar_tensor_tensor(
-                out=result, in0=banks[i][:], scalar=bias[:], in1=picked_gates[:, cols], op0=ADD, op1=MULT
-            )
+            late = starts[i] - (S - LATE)
+            gate = picked_gates[:, cols] if late < 0 else landing[1][:, late : late + WIDTHS[i]]
+            nc.vector.scalar_tensor_tensor(out=result, in0=banks[i][:], scalar=bias[:], in1=gate, op0=ADD, op1=MULT)
             nc.sync.dma_start(out=out[:, cols], in_=result)
 
         def result_tile(width, held_by):
             return keep.tile([P, width], F32, name="result%d" % held_by, tag="shared%d" % held_by)
 
-        nc.vector.tensor_copy(picked_gates[:], gates[:].indirect(offsets[:]))
+        split = (S - LATE) // PER_COL
+        nc.vector.tensor_copy(picked_gates[:], gates[:].indirect(offsets[:, 0:split]))
 
         last = len(WIDTHS) - 1
         round_chunk(0)
-        for i in range(last - 1):
-            round_chunk(i + 1)
-            multiply(i)
-            if i > 0:
-                finish(i - 1, result_tile(WIDTHS[i - 1], i)[:])
+        multiply(0)
+        round_chunk(1)
+        nc.vector.tensor_copy(landing[1][:, 0:LATE], gates[:].indirect(offsets[:, split:]))
+        multiply(1)
+        for i in range(2, last):
+            round_chunk(i)
+            finish(i - 2, landing[i][:, 0 : WIDTHS[i - 2]])
+            if i < last - 1:
+                multiply(i)
         round_chunk(last)
         multiply(last - 1)
         multiply(last)

@@ -20,11 +20,11 @@ P = 128
 PACK = 4
 PER_COL = 16
 SCALE_ROWS = K // 32
-STAGE_FROM, STAGE_STEP = 32, 4
+STAGED = P - SCALE_ROWS
 QUADRANT = 32
 
 WIDTHS = [256] + [512] * 2 + [256] * 2 + [128] * 2
-ON_VECTOR = {1: 128, 2: 192, 4: 96, 6: 64}
+ON_VECTOR = {1: 128, 2: 256, 4: 96, 6: 64}
 FIRST = 32
 LATE = 512
 OVERLAP = 16
@@ -55,18 +55,16 @@ def tile_list_tabgate_bias_kernel(tc, tab_words, tab_scales, w4_words, w4_scales
         picked_gates = keep.tile([P, S - LATE], F32, name="picked_gates")
 
         nc.vector.memset(w4_plane[:], 0)
-        nc.vector.memset(tab_rows[:], 0)
+        nc.vector.memset(tab_rows[0:STAGED, :], 0)
         nc.vector.memset(picked_plane[:], 0)
 
-        staged = slice(STAGE_FROM, STAGE_FROM + STAGE_STEP * SCALE_ROWS, STAGE_STEP)
+        nc.sync.dma_start(out=tab_rows[STAGED:P, :], in_=tab_scales[0].bitcast(I32))
         nc.sync.dma_start(offsets[:], offs)
-        nc.sync.dma_start(out=u_raw[:], in_=u.rearrange("(p t) n -> p t n", t=PACK))
-        w4_rows = w4_scales[0].bitcast(I32)
-        nc.sync.dma_start(out=w4_plane[0:P:QUADRANT, :], in_=w4_rows[0:SCALE_ROWS:4, :])
-        nc.sync.dma_start(out=tab_rows[staged, :], in_=tab_scales[0].bitcast(I32))
         nc.sync.dma_start(out=tab_codes[:], in_=tab_words[0].rearrange("p t i -> p (t i)").bitcast(I32))
+        nc.sync.dma_start(out=u_raw[:], in_=u.rearrange("(p t) n -> p t n", t=PACK))
         nc.sync.dma_start(out=w4_codes[:], in_=w4_words[0].bitcast(I32))
-        for r in range(1, 4):
+        w4_rows = w4_scales[0].bitcast(I32)
+        for r in range(4):
             nc.sync.dma_start(out=w4_plane[r:P:QUADRANT, :], in_=w4_rows[r:SCALE_ROWS:4, :])
         nc.sync.dma_start(out=gates[:], in_=gT)
         with nc.allow_non_contiguous_dma(reason="one bias value a partition"):
@@ -74,9 +72,7 @@ def tile_list_tabgate_bias_kernel(tc, tab_words, tab_scales, w4_words, w4_scales
 
         nc.vector.tensor_copy(picked_rows[:], tab_rows[:].bitcast(U8).indirect(offsets[:]))
         for r in range(4):
-            first = STAGE_FROM + STAGE_STEP * r
-            rows = slice(first, first + STAGE_STEP * SCALE_ROWS, 4 * STAGE_STEP)
-            nc.sync.dma_start(out=picked_plane[r:P:QUADRANT, :], in_=picked_rows[rows, :].bitcast(I32))
+            nc.sync.dma_start(out=picked_plane[r:P:QUADRANT, :], in_=picked_rows[STAGED + r : P : 4, :].bitcast(I32))
         c_rows = c.rearrange("(p t) j -> p t j", t=PACK)
         for i in chunks:
             nc.sync.dma_start(out=c_raw[i], in_=c_rows[:, :, starts[i] : starts[i + 1]])

@@ -24,7 +24,7 @@ STAGED = P - SCALE_ROWS
 QUADRANT = 32
 
 WIDTHS = [256] + [512] * 2 + [256] * 2 + [128] * 2
-ON_VECTOR = {1: 128, 2: 256, 4: 96, 6: 64}
+ON_VECTOR = {1: 224, 2: 288, 4: 48, 6: 64}
 FIRST = 32
 LATE = 512
 OVERLAP = 16
@@ -47,7 +47,7 @@ def tile_list_tabgate_bias_kernel(tc, tab_words, tab_scales, w4_words, w4_scales
         u_raw = keep.tile([P, PACK, M], F32, name="u_raw")
         bias = keep.tile([P, 1], F32, name="bias")
         gates = keep.tile([P, T], F32, name="gates")
-        ahead = [0, LATE - OVERLAP] + [WIDTHS[i - 2] - OVERLAP for i in range(2, len(WIDTHS) - 1)] + [0]
+        ahead = [0, LATE - OVERLAP, WIDTHS[0] - OVERLAP, 0, 0, 0, 0]
         landing = [keep.tile([P, ahead[i] + PACK * WIDTHS[i]], F32, name="landing%d" % i, tag="shared%d" % i) for i in chunks]
         c_raw = [landing[i][:, ahead[i] :].rearrange("p (t j) -> p t j", t=PACK) for i in chunks]
         picked_rows = keep.tile([P, S], U8, name="picked_rows", align_bytes=64)
@@ -156,11 +156,14 @@ def tile_list_tabgate_bias_kernel(tc, tab_words, tab_scales, w4_words, w4_scales
         round_chunk(1)
         nc.vector.tensor_copy(landing[1][:, 0:LATE], gates[:].indirect(offsets[:, split:]))
         multiply(1)
-        for i in range(2, last):
+        for i in (2, 4):
             round_chunk(i)
-            finish(i - 2, landing[i][:, 0 : WIDTHS[i - 2]])
-            if i < last - 1:
-                multiply(i)
+            finish(i - 2, landing[2 if i == 2 else 3][:, 0 : WIDTHS[i - 2]])
+            multiply(i)
+            finish(i - 1, c_raw[i][:, 1, 0 : WIDTHS[i - 1]])
+            round_chunk(i + 1)
+            if i + 1 < last - 1:
+                multiply(i + 1)
         round_chunk(last)
         multiply(last - 1)
         multiply(last)

@@ -24,7 +24,7 @@ STAGED = P - SCALE_ROWS
 QUADRANT = 32
 
 WIDTHS = [256] + [512] * 2 + [256] * 2 + [128] * 2
-ON_VECTOR = {1: 224, 2: 288, 4: 48, 6: 64}
+ON_VECTOR = {1: 224, 2: 288, 3: 64, 4: 96, 6: 64}
 FIRST = 32
 LATE = 512
 OVERLAP = 16
@@ -98,20 +98,23 @@ def tile_list_tabgate_bias_kernel(tc, tab_words, tab_scales, w4_words, w4_scales
         round_columns(nc.scalar.copy, u_grouped, u_raw, 0, M)
         quantise(u_grouped, 0, M)
 
-        banks = [psum.tile([P, WIDTHS[i]], F32, name="bank%d" % i) for i in chunks]
-        for i in chunks:
-            n = 512 if WIDTHS[i] == 512 else 128
-            for at in range(0, WIDTHS[i], n):
-                cols = slice(starts[i] + at, starts[i] + at + n)
-                nc.tensor.matmul_mx(
-                    out=banks[i][:, at : at + n],
-                    lhsT=w4_codes[:].bitcast(FP4X4),
-                    lhsT_scale=w4_plane[:].bitcast(U8),
-                    rhs=picked_codes[:, cols].bitcast(FP8X4),
-                    rhs_scale=picked_plane[:].bitcast(U8)[:, cols],
-                    start=(at == 0),
-                    stop=False,
-                )
+        banks = {}
+
+        def open_bank(i):
+            banks[i] = psum.tile([P, WIDTHS[i]], F32, name="bank%d" % i, tag="bank%d" % (i % 2 if i < len(WIDTHS) - 1 else 2))
+            cols = slice(starts[i], starts[i + 1])
+            nc.tensor.matmul_mx(
+                out=banks[i][:],
+                lhsT=w4_codes[:].bitcast(FP4X4),
+                lhsT_scale=w4_plane[:].bitcast(U8),
+                rhs=picked_codes[:, cols].bitcast(FP8X4),
+                rhs_scale=picked_plane[:].bitcast(U8)[:, cols],
+                start=True,
+                stop=False,
+            )
+
+        for i in (0, 1, len(WIDTHS) - 1):
+            open_bank(i)
 
         grouped = [keep.tile([P, WIDTHS[i], PACK], BF16, name="grouped%d" % i, align_bytes=64) for i in chunks]
 
@@ -143,6 +146,8 @@ def tile_list_tabgate_bias_kernel(tc, tab_words, tab_scales, w4_words, w4_scales
             gate = picked_gates[:, cols] if late < 0 else landing[1][:, late : late + WIDTHS[i]]
             nc.vector.scalar_tensor_tensor(out=result, in0=banks[i][:], scalar=bias[:], in1=gate, op0=ADD, op1=MULT)
             nc.sync.dma_start(out=out[:, cols], in_=result)
+            if i + 2 < len(WIDTHS) - 1:
+                open_bank(i + 2)
 
         def result_tile(width, held_by):
             return keep.tile([P, width], F32, name="result%d" % held_by, tag="shared%d" % held_by)
@@ -156,18 +161,20 @@ def tile_list_tabgate_bias_kernel(tc, tab_words, tab_scales, w4_words, w4_scales
         round_chunk(1)
         nc.vector.tensor_copy(landing[1][:, 0:LATE], gates[:].indirect(offsets[:, split:]))
         multiply(1)
-        for i in (2, 4):
-            round_chunk(i)
-            finish(i - 2, landing[2 if i == 2 else 3][:, 0 : WIDTHS[i - 2]])
-            multiply(i)
-            finish(i - 1, c_raw[i][:, 1, 0 : WIDTHS[i - 1]])
-            round_chunk(i + 1)
-            if i + 1 < last - 1:
-                multiply(i + 1)
-        round_chunk(last)
-        multiply(last - 1)
-        multiply(last)
-        held = result_tile(WIDTHS[last - 2] + WIDTHS[last - 1], last)
-        finish(last - 2, held[:, 0 : WIDTHS[last - 2]])
-        finish(last - 1, held[:, WIDTHS[last - 2] :])
-        finish(last, result_tile(WIDTHS[last], last + 1)[:])
+        round_chunk(2)
+        finish(0, landing[2][:, 0 : WIDTHS[0]])
+        multiply(2)
+        round_chunk(3)
+        finish(1, c_raw[2][:, 1, :])
+        multiply(3)
+        round_chunk(4)
+        finish(2, landing[3][:, 0 : WIDTHS[2]])
+        multiply(4)
+        finish(3, c_raw[4][:, 1, :])
+        round_chunk(5)
+        multiply(5)
+        round_chunk(6)
+        finish(4, result_tile(WIDTHS[4], last + 1)[:])
+        multiply(6)
+        finish(5, result_tile(WIDTHS[5], last + 2)[:])
+        finish(6, result_tile(WIDTHS[6], last + 3)[:])

@@ -23,16 +23,17 @@ SCALE_ROWS = K // 32
 STAGED = P - SCALE_ROWS
 QUADRANT = 32
 
-WIDTHS = [256] + [512] * 2 + [256] * 2 + [128] * 2
-ON_VECTOR = {1: 224, 2: 288, 3: 64, 4: 96, 6: 64}
+WIDTHS = [512, 512, 256, 256, 256, 128, 128]
+ON_VECTOR = {0: 256, 1: 192, 2: 64, 3: 32, 4: 160, 6: 64}
+SHORT_FIRST = []
 FIRST = 32
-LATE = 512
 OVERLAP = 16
 
 
 def tile_list_tabgate_bias_kernel(tc, tab_words, tab_scales, w4_words, w4_scales, c, u, gT, b, offs, out):
     nc = tc.nc
     chunks = range(len(WIDTHS))
+    last = len(WIDTHS) - 1
     starts = [sum(WIDTHS[:i]) for i in range(len(WIDTHS) + 1)]
     with ExitStack() as ctx:
         keep = ctx.enter_context(tc.tile_pool(name="keep", bufs=1))
@@ -47,41 +48,52 @@ def tile_list_tabgate_bias_kernel(tc, tab_words, tab_scales, w4_words, w4_scales
         u_raw = keep.tile([P, PACK, M], F32, name="u_raw")
         bias = keep.tile([P, 1], F32, name="bias")
         gates = keep.tile([P, T], F32, name="gates")
-        ahead = [0, LATE - OVERLAP, WIDTHS[0] - OVERLAP, 0, 0, 0, 0]
-        landing = [keep.tile([P, ahead[i] + PACK * WIDTHS[i]], F32, name="landing%d" % i, tag="shared%d" % i) for i in chunks]
-        c_raw = [landing[i][:, ahead[i] :].rearrange("p (t j) -> p t j", t=PACK) for i in chunks]
+        c_flat = keep.tile([P, PACK * S], F32, name="c_flat")
+        c_raw = c_flat[:].rearrange("p (t j) -> p t j", t=PACK)
         picked_rows = keep.tile([P, S], U8, name="picked_rows", align_bytes=64)
         picked_codes = keep.tile([P, S], U32, name="picked_codes", align_bytes=64)
-        picked_gates = keep.tile([P, S - LATE], F32, name="picked_gates")
+        picked_gates = keep.tile([P, S], F32, name="picked_gates")
 
         nc.vector.memset(w4_plane[:], 0)
         nc.vector.memset(tab_rows[0:STAGED, :], 0)
         nc.vector.memset(picked_plane[:], 0)
 
+        w4_rows = w4_scales[0].bitcast(I32)
+        c_rows = c.rearrange("(p t) j -> p t j", t=PACK)
+
+        def load_c(rows, cols):
+            nc.sync.dma_start(out=c_raw[:, rows, cols], in_=c_rows[:, rows, cols])
+
         nc.sync.dma_start(out=tab_rows[STAGED:P, :], in_=tab_scales[0].bitcast(I32))
         nc.sync.dma_start(offsets[:], offs)
         nc.sync.dma_start(out=tab_codes[:], in_=tab_words[0].rearrange("p t i -> p (t i)").bitcast(I32))
-        nc.sync.dma_start(out=u_raw[:], in_=u.rearrange("(p t) n -> p t n", t=PACK))
-        nc.sync.dma_start(out=w4_codes[:], in_=w4_words[0].bitcast(I32))
-        w4_rows = w4_scales[0].bitcast(I32)
         for r in range(4):
             nc.sync.dma_start(out=w4_plane[r:P:QUADRANT, :], in_=w4_rows[r:SCALE_ROWS:4, :])
+        nc.sync.dma_start(out=w4_codes[:], in_=w4_words[0].bitcast(I32))
         nc.sync.dma_start(out=gates[:], in_=gT)
-        with nc.allow_non_contiguous_dma(reason="one bias value a partition"):
-            nc.sync.dma_start(out=bias[:], in_=b.rearrange("(p o) -> p o", o=1))
-
+        nc.sync.dma_start(out=u_raw[:], in_=u.rearrange("(p t) n -> p t n", t=PACK))
+        load_c(slice(0, 2), slice(0, 1024))
+        load_c(slice(2, 4), slice(0, 512))
+        load_c(slice(2, 4), slice(512, 1024))
         nc.vector.tensor_copy(picked_rows[:], tab_rows[:].bitcast(U8).indirect(offsets[:]))
         for r in range(4):
             nc.sync.dma_start(out=picked_plane[r:P:QUADRANT, :], in_=picked_rows[STAGED + r : P : 4, :].bitcast(I32))
-        c_rows = c.rearrange("(p t) j -> p t j", t=PACK)
-        for i in chunks:
-            nc.sync.dma_start(out=c_raw[i], in_=c_rows[:, :, starts[i] : starts[i + 1]])
+        with nc.allow_non_contiguous_dma(reason="one bias value a partition"):
+            nc.sync.dma_start(out=bias[:], in_=b.rearrange("(p o) -> p o", o=1))
+        load_c(slice(0, 1), slice(1024, 2048))
+        load_c(slice(1, 4), slice(1024, 1280))
+        load_c(slice(1, 4), slice(1280, 1536))
+        load_c(slice(1, 4), slice(1536, 1792))
+        load_c(slice(1, 4), slice(1792, 1920))
+        load_c(slice(1, 4), slice(1920, 2048))
+
         nc.vector.tensor_copy(picked_codes[:], tab_codes[:].bitcast(U32).indirect(offsets[:]))
+        nc.vector.tensor_copy(picked_gates[:], gates[:].indirect(offsets[:]))
 
         def round_columns(engine_copy, grouped, raw, lo, hi):
             engine_copy(
-                out=grouped[:, lo:hi, :].rearrange("p (a i) t -> p a t i", i=2),
-                in_=raw[:, :, lo:hi].rearrange("p t (a i) -> p a t i", i=2),
+                out=grouped[:, lo:hi, :],
+                in_=raw[:, :, lo:hi].rearrange("p t j -> p j t"),
             )
 
         codes = keep.tile([P, M + S], U32, name="codes", align_bytes=64)
@@ -94,14 +106,10 @@ def tile_list_tabgate_bias_kernel(tc, tab_words, tab_scales, w4_words, w4_scales
                 in_=grouped[:].rearrange("p j t -> p (j t)"),
             )
 
-        u_grouped = keep.tile([P, M, PACK], BF16, name="u_grouped", align_bytes=64)
-        round_columns(nc.scalar.copy, u_grouped, u_raw, 0, M)
-        quantise(u_grouped, 0, M)
-
         banks = {}
 
         def open_bank(i):
-            banks[i] = psum.tile([P, WIDTHS[i]], F32, name="bank%d" % i, tag="bank%d" % (i % 2 if i < len(WIDTHS) - 1 else 2))
+            banks[i] = psum.tile([P, WIDTHS[i]], F32, name="bank%d" % i, tag="bank%d" % (i % 3 if i < last else 3))
             cols = slice(starts[i], starts[i + 1])
             nc.tensor.matmul_mx(
                 out=banks[i][:],
@@ -113,23 +121,23 @@ def tile_list_tabgate_bias_kernel(tc, tab_words, tab_scales, w4_words, w4_scales
                 stop=False,
             )
 
-        for i in (0, 1, len(WIDTHS) - 1):
+        for i in (0, 1, 2, last):
             open_bank(i)
 
+        u_grouped = keep.tile([P, M, PACK], BF16, name="u_grouped", align_bytes=64)
         grouped = [keep.tile([P, WIDTHS[i], PACK], BF16, name="grouped%d" % i, align_bytes=64) for i in chunks]
 
         def round_chunk(i):
             on_scalar = WIDTHS[i] - ON_VECTOR.get(i, 0)
-            first = FIRST if ahead[i] > 0 else 0
+            first = FIRST if i in SHORT_FIRST else 0
             if first > 0:
-                round_columns(nc.scalar.copy, grouped[i], c_raw[i], 0, first)
-            round_columns(nc.scalar.copy, grouped[i], c_raw[i], first, on_scalar)
+                round_columns(nc.scalar.copy, grouped[i], c_raw[:, :, starts[i] : starts[i + 1]], 0, first)
+            round_columns(nc.scalar.copy, grouped[i], c_raw[:, :, starts[i] : starts[i + 1]], first, on_scalar)
             if on_scalar < WIDTHS[i]:
-                round_columns(nc.vector.tensor_copy, grouped[i], c_raw[i], on_scalar, WIDTHS[i])
+                round_columns(nc.vector.tensor_copy, grouped[i], c_raw[:, :, starts[i] : starts[i + 1]], on_scalar, WIDTHS[i])
 
-        def multiply(i):
+        def close_bank(i):
             lo, hi = M + starts[i], M + starts[i + 1]
-            quantise(grouped[i], lo, hi)
             nc.tensor.matmul_mx(
                 out=banks[i][:],
                 lhsT=codes[:, 0:M].bitcast(FP8X4),
@@ -142,39 +150,41 @@ def tile_list_tabgate_bias_kernel(tc, tab_words, tab_scales, w4_words, w4_scales
 
         def finish(i, result):
             cols = slice(starts[i], starts[i + 1])
-            late = starts[i] - (S - LATE)
-            gate = picked_gates[:, cols] if late < 0 else landing[1][:, late : late + WIDTHS[i]]
-            nc.vector.scalar_tensor_tensor(out=result, in0=banks[i][:], scalar=bias[:], in1=gate, op0=ADD, op1=MULT)
+            nc.vector.scalar_tensor_tensor(out=result, in0=banks[i][:], scalar=bias[:], in1=picked_gates[:, cols], op0=ADD, op1=MULT)
             nc.sync.dma_start(out=out[:, cols], in_=result)
-            if i + 2 < len(WIDTHS) - 1:
-                open_bank(i + 2)
+            if i + 3 < last:
+                open_bank(i + 3)
 
-        def result_tile(width, held_by):
-            return keep.tile([P, width], F32, name="result%d" % held_by, tag="shared%d" % held_by)
+        def held_by(i, row, width):
+            return c_raw[:, row, starts[i] + OVERLAP - width : starts[i] + OVERLAP]
 
-        split = (S - LATE) // PER_COL
-        nc.vector.tensor_copy(picked_gates[:], gates[:].indirect(offsets[:, 0:split]))
-
-        last = len(WIDTHS) - 1
+        round_columns(nc.scalar.copy, u_grouped, u_raw, 0, M)
+        quantise(u_grouped, 0, M)
         round_chunk(0)
-        multiply(0)
         round_chunk(1)
-        nc.vector.tensor_copy(landing[1][:, 0:LATE], gates[:].indirect(offsets[:, split:]))
-        multiply(1)
+        quantise(grouped[0], M + starts[0], M + starts[0 + 1])
+        close_bank(0)
+        quantise(grouped[1], M + starts[1], M + starts[1 + 1])
+        close_bank(1)
+        finish(0, keep.tile([P, WIDTHS[0]], F32, name="result0")[:])
+        finish(1, keep.tile([P, WIDTHS[1]], F32, name="result1")[:])
         round_chunk(2)
-        finish(0, landing[2][:, 0 : WIDTHS[0]])
-        multiply(2)
         round_chunk(3)
-        finish(1, c_raw[2][:, 1, :])
-        multiply(3)
+        quantise(grouped[2], M + starts[2], M + starts[2 + 1])
+        close_bank(2)
         round_chunk(4)
-        finish(2, landing[3][:, 0 : WIDTHS[2]])
-        multiply(4)
-        finish(3, c_raw[4][:, 1, :])
+        quantise(grouped[3], M + starts[3], M + starts[3 + 1])
+        close_bank(3)
+        finish(2, held_by(3, 2, WIDTHS[2]))
+        quantise(grouped[4], M + starts[4], M + starts[4 + 1])
+        close_bank(4)
         round_chunk(5)
-        multiply(5)
         round_chunk(6)
-        finish(4, result_tile(WIDTHS[4], last + 1)[:])
-        multiply(6)
-        finish(5, result_tile(WIDTHS[5], last + 2)[:])
-        finish(6, result_tile(WIDTHS[6], last + 3)[:])
+        quantise(grouped[5], M + starts[5], M + starts[5 + 1])
+        close_bank(5)
+        finish(3, held_by(5, 0, WIDTHS[3]))
+        quantise(grouped[6], M + starts[6], M + starts[6 + 1])
+        close_bank(6)
+        finish(4, held_by(6, 3, WIDTHS[4]))
+        finish(5, keep.tile([P, WIDTHS[5]], F32, name="result5")[:])
+        finish(6, keep.tile([P, WIDTHS[6]], F32, name="result6")[:])

@@ -62,7 +62,10 @@ def tile_list_tabgate_bias_kernel(tc, tab_words, tab_scales, w4_words, w4_scales
         c_rows = c.rearrange("(p t) j -> p t j", t=PACK)
 
         def load_c(rows, cols):
-            nc.sync.dma_start(out=c_raw[:, rows, cols], in_=c_rows[:, rows, cols])
+            nc.sync.dma_start(
+                out=c_raw[:, rows, cols].rearrange("p t (a i) -> p t a i", i=2),
+                in_=c_rows[:, rows, cols].rearrange("p t (a i) -> p t a i", i=2),
+            )
 
         nc.sync.dma_start(out=tab_rows[STAGED:P, :], in_=tab_scales[0].bitcast(I32))
         nc.sync.dma_start(offsets[:], offs)
@@ -92,8 +95,8 @@ def tile_list_tabgate_bias_kernel(tc, tab_words, tab_scales, w4_words, w4_scales
 
         def round_columns(engine_copy, grouped, raw, lo, hi):
             engine_copy(
-                out=grouped[:, lo:hi, :],
-                in_=raw[:, :, lo:hi].rearrange("p t j -> p j t"),
+                out=grouped[:, lo:hi, :].rearrange("p (a i) t -> p a t i", i=2),
+                in_=raw[:, :, lo:hi].rearrange("p t (a i) -> p a t i", i=2),
             )
 
         codes = keep.tile([P, M + S], U32, name="codes", align_bytes=64)
@@ -175,7 +178,7 @@ def tile_list_tabgate_bias_kernel(tc, tab_words, tab_scales, w4_words, w4_scales
         round_chunk(4)
         quantise(grouped[3], M + starts[3], M + starts[3 + 1])
         close_bank(3)
-        finish(2, held_by(3, 2, WIDTHS[2]))
+        finish(2, held_by(3, 0, WIDTHS[2]))
         quantise(grouped[4], M + starts[4], M + starts[4 + 1])
         close_bank(4)
         round_chunk(5)

@@ -48,8 +48,8 @@ def tile_list_tabgate_bias_kernel(tc, tab_words, tab_scales, w4_words, w4_scales
         u_raw = keep.tile([P, PACK, M], F32, name="u_raw")
         bias = keep.tile([P, 1], F32, name="bias")
         gates = keep.tile([P, T], F32, name="gates")
-        c_flat = keep.tile([P, PACK * S], F32, name="c_flat")
-        c_raw = c_flat[:].rearrange("p (t j) -> p t j", t=PACK)
+        c_flat = keep.tile([P, PACK * (S + 16)], F32, name="c_flat")
+        c_raw = c_flat[:].rearrange("p (t j) -> p t j", t=PACK)[:, :, 0:S]
         picked_rows = keep.tile([P, S], U8, name="picked_rows", align_bytes=64)
         picked_codes = keep.tile([P, S], U32, name="picked_codes", align_bytes=64)
         picked_gates = keep.tile([P, S], F32, name="picked_gates")

@@ -23,11 +23,14 @@ SCALE_ROWS = K // 32
 STAGED = P - SCALE_ROWS
 QUADRANT = 32
 
-WIDTHS = [512, 512, 256, 256, 256, 128, 128]
-ON_VECTOR = {0: 256, 1: 192, 2: 64, 3: 32, 4: 160, 6: 64}
-SHORT_FIRST = []
+WIDTHS = [512] * 2 + [256] * 3 + [128] * 2
+WIDE = 2
+HALF = S // 2
+ON_VECTOR = {1: 64, 2: 64, 4: 160, 6: 64}
 FIRST = 32
 OVERLAP = 16
+PAD = 16
+BANKS = 3
 
 
 def tile_list_tabgate_bias_kernel(tc, tab_words, tab_scales, w4_words, w4_scales, c, u, gT, b, offs, out):
@@ -48,8 +51,11 @@ def tile_list_tabgate_bias_kernel(tc, tab_words, tab_scales, w4_words, w4_scales
         u_raw = keep.tile([P, PACK, M], F32, name="u_raw")
         bias = keep.tile([P, 1], F32, name="bias")
         gates = keep.tile([P, T], F32, name="gates")
-        c_flat = keep.tile([P, PACK * (S + 16)], F32, name="c_flat")
-        c_raw = c_flat[:].rearrange("p (t j) -> p t j", t=PACK)[:, :, 0:S]
+        wide = [keep.tile([P, PACK, WIDTHS[i] + PAD], F32, name="wide%d" % i) for i in range(WIDE)]
+        ahead = WIDTHS[WIDE - 1] - OVERLAP
+        second = keep.tile([P, ahead + PACK * (HALF + PAD)], F32, name="second")
+        second_rows = second[:, ahead:].rearrange("p (t j) -> p t j", t=PACK)
+        c_raw = [wide[i][:, :, 0 : WIDTHS[i]] if i < WIDE else second_rows[:, :, starts[i] - HALF : starts[i + 1] - HALF] for i in chunks]
         picked_rows = keep.tile([P, S], U8, name="picked_rows", align_bytes=64)
         picked_codes = keep.tile([P, S], U32, name="picked_codes", align_bytes=64)
         picked_gates = keep.tile([P, S], F32, name="picked_gates")
@@ -61,10 +67,10 @@ def tile_list_tabgate_bias_kernel(tc, tab_words, tab_scales, w4_words, w4_scales
         w4_rows = w4_scales[0].bitcast(I32)
         c_rows = c.rearrange("(p t) j -> p t j", t=PACK)
 
-        def load_c(rows, cols):
+        def load_c(tile_rows, hbm_rows):
             nc.sync.dma_start(
-                out=c_raw[:, rows, cols].rearrange("p t (a i) -> p t a i", i=2),
-                in_=c_rows[:, rows, cols].rearrange("p t (a i) -> p t a i", i=2),
+                out=tile_rows.rearrange("p t (a i) -> p t a i", i=2),
+                in_=hbm_rows.rearrange("p t (a i) -> p t a i", i=2),
             )
 
         nc.sync.dma_start(out=tab_rows[STAGED:P, :], in_=tab_scales[0].bitcast(I32))
@@ -75,20 +81,16 @@ def tile_list_tabgate_bias_kernel(tc, tab_words, tab_scales, w4_words, w4_scales
         nc.sync.dma_start(out=w4_codes[:], in_=w4_words[0].bitcast(I32))
         nc.sync.dma_start(out=gates[:], in_=gT)
         nc.sync.dma_start(out=u_raw[:], in_=u.rearrange("(p t) n -> p t n", t=PACK))
-        load_c(slice(0, 2), slice(0, 1024))
-        load_c(slice(2, 4), slice(0, 512))
-        load_c(slice(2, 4), slice(512, 1024))
+        for i in range(WIDE):
+            load_c(c_raw[i], c_rows[:, :, starts[i] : starts[i + 1]])
         nc.vector.tensor_copy(picked_rows[:], tab_rows[:].bitcast(U8).indirect(offsets[:]))
         for r in range(4):
             nc.sync.dma_start(out=picked_plane[r:P:QUADRANT, :], in_=picked_rows[STAGED + r : P : 4, :].bitcast(I32))
         with nc.allow_non_contiguous_dma(reason="one bias value a partition"):
             nc.sync.dma_start(out=bias[:], in_=b.rearrange("(p o) -> p o", o=1))
-        load_c(slice(0, 1), slice(1024, 2048))
-        load_c(slice(1, 4), slice(1024, 1280))
-        load_c(slice(1, 4), slice(1280, 1536))
-        load_c(slice(1, 4), slice(1536, 1792))
-        load_c(slice(1, 4), slice(1792, 1920))
-        load_c(slice(1, 4), slice(1920, 2048))
+        load_c(second_rows[:, 0:1, 0:HALF], c_rows[:, 0:1, HALF:S])
+        for i in chunks[WIDE:]:
+            load_c(c_raw[i][:, 1:PACK, :], c_rows[:, 1:PACK, starts[i] : starts[i + 1]])
 
         nc.vector.tensor_copy(picked_codes[:], tab_codes[:].bitcast(U32).indirect(offsets[:]))
         nc.vector.tensor_copy(picked_gates[:], gates[:].indirect(offsets[:]))
@@ -101,18 +103,19 @@ def tile_list_tabgate_bias_kernel(tc, tab_words, tab_scales, w4_words, w4_scales
 
         codes = keep.tile([P, M + S], U32, name="codes", align_bytes=64)
         plane = keep.tile([P, M + S], U8, name="plane", align_bytes=64)
+        u_grouped = keep.tile([P, M, PACK], BF16, name="u_grouped", align_bytes=64)
+        grouped = [keep.tile([P, WIDTHS[i], PACK], BF16, name="grouped%d" % i, align_bytes=64) for i in chunks]
+        banks = {}
 
-        def quantise(grouped, lo, hi):
+        def quantise(rounded, lo, hi):
             nc.vector.quantize_mx(
                 out=codes[:, lo:hi].bitcast(FP8X4),
                 scales=plane[:, lo:hi],
-                in_=grouped[:].rearrange("p j t -> p (j t)"),
+                in_=rounded[:].rearrange("p j t -> p (j t)"),
             )
 
-        banks = {}
-
         def open_bank(i):
-            banks[i] = psum.tile([P, WIDTHS[i]], F32, name="bank%d" % i, tag="bank%d" % (i % 3 if i < last else 3))
+            banks[i] = psum.tile([P, WIDTHS[i]], F32, name="bank%d" % i, tag="bank%d" % (i % BANKS if i < last else BANKS))
             cols = slice(starts[i], starts[i + 1])
             nc.tensor.matmul_mx(
                 out=banks[i][:],
@@ -124,23 +127,17 @@ def tile_list_tabgate_bias_kernel(tc, tab_words, tab_scales, w4_words, w4_scales
                 stop=False,
             )
 
-        for i in (0, 1, 2, last):
-            open_bank(i)
-
-        u_grouped = keep.tile([P, M, PACK], BF16, name="u_grouped", align_bytes=64)
-        grouped = [keep.tile([P, WIDTHS[i], PACK], BF16, name="grouped%d" % i, align_bytes=64) for i in chunks]
-
-        def round_chunk(i):
+        def round_chunk(i, first=0):
             on_scalar = WIDTHS[i] - ON_VECTOR.get(i, 0)
-            first = FIRST if i in SHORT_FIRST else 0
             if first > 0:
-                round_columns(nc.scalar.copy, grouped[i], c_raw[:, :, starts[i] : starts[i + 1]], 0, first)
-            round_columns(nc.scalar.copy, grouped[i], c_raw[:, :, starts[i] : starts[i + 1]], first, on_scalar)
+                round_columns(nc.scalar.copy, grouped[i], c_raw[i], 0, first)
+            round_columns(nc.scalar.copy, grouped[i], c_raw[i], first, on_scalar)
             if on_scalar < WIDTHS[i]:
-                round_columns(nc.vector.tensor_copy, grouped[i], c_raw[:, :, starts[i] : starts[i + 1]], on_scalar, WIDTHS[i])
+                round_columns(nc.vector.tensor_copy, grouped[i], c_raw[i], on_scalar, WIDTHS[i])
 
-        def close_bank(i):
+        def multiply(i):
             lo, hi = M + starts[i], M + starts[i + 1]
+            quantise(grouped[i], lo, hi)
             nc.tensor.matmul_mx(
                 out=banks[i][:],
                 lhsT=codes[:, 0:M].bitcast(FP8X4),
@@ -155,39 +152,40 @@ def tile_list_tabgate_bias_kernel(tc, tab_words, tab_scales, w4_words, w4_scales
             cols = slice(starts[i], starts[i + 1])
             nc.vector.scalar_tensor_tensor(out=result, in0=banks[i][:], scalar=bias[:], in1=picked_gates[:, cols], op0=ADD, op1=MULT)
             nc.sync.dma_start(out=out[:, cols], in_=result)
-            if i + 3 < last:
-                open_bank(i + 3)
+            if i + BANKS < last:
+                open_bank(i + BANKS)
+
+        def own_tile(i):
+            return keep.tile([P, WIDTHS[i]], F32, name="result%d" % i)[:]
 
         def held_by(i, row, width):
-            return c_raw[:, row, starts[i] + OVERLAP - width : starts[i] + OVERLAP]
+            end = ahead + row * (HALF + PAD) + starts[i] - HALF + OVERLAP
+            return second[:, end - width : end]
 
+        open_bank(0)
+        open_bank(1)
         round_columns(nc.scalar.copy, u_grouped, u_raw, 0, M)
         quantise(u_grouped, 0, M)
         round_chunk(0)
+        multiply(0)
+        open_bank(2)
+        open_bank(6)
         round_chunk(1)
-        quantise(grouped[0], M + starts[0], M + starts[0 + 1])
-        close_bank(0)
-        quantise(grouped[1], M + starts[1], M + starts[1 + 1])
-        close_bank(1)
-        finish(0, keep.tile([P, WIDTHS[0]], F32, name="result0")[:])
-        finish(1, keep.tile([P, WIDTHS[1]], F32, name="result1")[:])
-        round_chunk(2)
+        multiply(1)
+        finish(0, own_tile(0))
+        round_chunk(2, FIRST)
+        finish(1, held_by(2, 0, WIDTHS[1]))
+        multiply(2)
         round_chunk(3)
-        quantise(grouped[2], M + starts[2], M + starts[2 + 1])
-        close_bank(2)
         round_chunk(4)
-        quantise(grouped[3], M + starts[3], M + starts[3 + 1])
-        close_bank(3)
+        multiply(3)
         finish(2, held_by(3, 0, WIDTHS[2]))
-        quantise(grouped[4], M + starts[4], M + starts[4 + 1])
-        close_bank(4)
+        multiply(4)
         round_chunk(5)
         round_chunk(6)
-        quantise(grouped[5], M + starts[5], M + starts[5 + 1])
-        close_bank(5)
+        multiply(5)
         finish(3, held_by(5, 0, WIDTHS[3]))
-        quantise(grouped[6], M + starts[6], M + starts[6 + 1])
-        close_bank(6)
+        multiply(6)
         finish(4, held_by(6, 3, WIDTHS[4]))
-        finish(5, keep.tile([P, WIDTHS[5]], F32, name="result5")[:])
-        finish(6, keep.tile([P, WIDTHS[6]], F32, name="result6")[:])
+        finish(5, own_tile(5))
+        finish(6, own_tile(6))

@@ -24,9 +24,9 @@ STAGED = P - SCALE_ROWS
 QUADRANT = 32
 
 WIDTHS = [512] * 2 + [256] * 3 + [128] * 2
-WIDE = 2
-HALF = S // 2
-ON_VECTOR = {1: 64, 2: 64, 4: 160, 6: 64}
+SHARED = range(2, 5)
+ON_VECTOR = {1: 176, 2: 112, 3: 80, 4: 112, 6: 80}
+AHEAD = {2: 2, 3: 2, 4: 1}
 FIRST = 32
 OVERLAP = 16
 PAD = 16
@@ -51,11 +51,16 @@ def tile_list_tabgate_bias_kernel(tc, tab_words, tab_scales, w4_words, w4_scales
         u_raw = keep.tile([P, PACK, M], F32, name="u_raw")
         bias = keep.tile([P, 1], F32, name="bias")
         gates = keep.tile([P, T], F32, name="gates")
-        wide = [keep.tile([P, PACK, WIDTHS[i] + PAD], F32, name="wide%d" % i) for i in range(WIDE)]
-        ahead = WIDTHS[WIDE - 1] - OVERLAP
-        second = keep.tile([P, ahead + PACK * (HALF + PAD)], F32, name="second")
-        second_rows = second[:, ahead:].rearrange("p (t j) -> p t j", t=PACK)
-        c_raw = [wide[i][:, :, 0 : WIDTHS[i]] if i < WIDE else second_rows[:, :, starts[i] - HALF : starts[i + 1] - HALF] for i in chunks]
+        base, span = starts[SHARED.start], starts[SHARED.stop] - starts[SHARED.start]
+        ahead = WIDTHS[SHARED.start - 1] - OVERLAP
+        middle = keep.tile([P, ahead + PACK * (span + PAD)], F32, name="middle")
+        middle_rows = middle[:, ahead:].rearrange("p (t j) -> p t j", t=PACK)
+        c_raw = [
+            middle_rows[:, :, starts[i] - base : starts[i + 1] - base]
+            if i in SHARED
+            else keep.tile([P, PACK, WIDTHS[i] + PAD], F32, name="landing%d" % i)[:, :, 0 : WIDTHS[i]]
+            for i in chunks
+        ]
         picked_rows = keep.tile([P, S], U8, name="picked_rows", align_bytes=64)
         picked_codes = keep.tile([P, S], U32, name="picked_codes", align_bytes=64)
         picked_gates = keep.tile([P, S], F32, name="picked_gates")
@@ -79,18 +84,21 @@ def tile_list_tabgate_bias_kernel(tc, tab_words, tab_scales, w4_words, w4_scales
         for r in range(4):
             nc.sync.dma_start(out=w4_plane[r:P:QUADRANT, :], in_=w4_rows[r:SCALE_ROWS:4, :])
         nc.sync.dma_start(out=w4_codes[:], in_=w4_words[0].bitcast(I32))
+        with nc.allow_non_contiguous_dma(reason="one bias value a partition"):
+            nc.sync.dma_start(out=bias[:], in_=b.rearrange("(p o) -> p o", o=1))
         nc.sync.dma_start(out=gates[:], in_=gT)
         nc.sync.dma_start(out=u_raw[:], in_=u.rearrange("(p t) n -> p t n", t=PACK))
-        for i in range(WIDE):
+        for i in range(SHARED.start):
             load_c(c_raw[i], c_rows[:, :, starts[i] : starts[i + 1]])
         nc.vector.tensor_copy(picked_rows[:], tab_rows[:].bitcast(U8).indirect(offsets[:]))
         for r in range(4):
             nc.sync.dma_start(out=picked_plane[r:P:QUADRANT, :], in_=picked_rows[STAGED + r : P : 4, :].bitcast(I32))
-        with nc.allow_non_contiguous_dma(reason="one bias value a partition"):
-            nc.sync.dma_start(out=bias[:], in_=b.rearrange("(p o) -> p o", o=1))
-        load_c(second_rows[:, 0:1, 0:HALF], c_rows[:, 0:1, HALF:S])
-        for i in chunks[WIDE:]:
-            load_c(c_raw[i][:, 1:PACK, :], c_rows[:, 1:PACK, starts[i] : starts[i + 1]])
+        for row in range(max(AHEAD.values())):
+            width = sum(WIDTHS[i] for i in SHARED if AHEAD[i] > row)
+            load_c(middle_rows[:, row : row + 1, 0:width], c_rows[:, row : row + 1, base : base + width])
+        for i in chunks[SHARED.start :]:
+            rows = slice(AHEAD.get(i, 0), PACK)
+            load_c(c_raw[i][:, rows, :], c_rows[:, rows, starts[i] : starts[i + 1]])
 
         nc.vector.tensor_copy(picked_codes[:], tab_codes[:].bitcast(U32).indirect(offsets[:]))
         nc.vector.tensor_copy(picked_gates[:], gates[:].indirect(offsets[:]))
@@ -159,33 +167,33 @@ def tile_list_tabgate_bias_kernel(tc, tab_words, tab_scales, w4_words, w4_scales
             return keep.tile([P, WIDTHS[i]], F32, name="result%d" % i)[:]
 
         def held_by(i, row, width):
-            end = ahead + row * (HALF + PAD) + starts[i] - HALF + OVERLAP
-            return second[:, end - width : end]
+            end = ahead + row * (span + PAD) + starts[i] - base + OVERLAP
+            return middle[:, end - width : end]
 
         open_bank(0)
-        open_bank(1)
         round_columns(nc.scalar.copy, u_grouped, u_raw, 0, M)
         quantise(u_grouped, 0, M)
         round_chunk(0)
         multiply(0)
+        open_bank(1)
         open_bank(2)
-        open_bank(6)
         round_chunk(1)
         multiply(1)
+        open_bank(6)
         finish(0, own_tile(0))
-        round_chunk(2, FIRST)
-        finish(1, held_by(2, 0, WIDTHS[1]))
-        multiply(2)
+        round_chunk(2)
         round_chunk(3)
-        round_chunk(4)
+        multiply(2)
+        finish(1, held_by(2, 0, WIDTHS[1]))
         multiply(3)
-        finish(2, held_by(3, 0, WIDTHS[2]))
+        round_chunk(4)
+        finish(2, own_tile(2))
         multiply(4)
+        finish(3, own_tile(3))
         round_chunk(5)
-        round_chunk(6)
         multiply(5)
-        finish(3, held_by(5, 0, WIDTHS[3]))
+        round_chunk(6)
+        finish(4, own_tile(4))
         multiply(6)
-        finish(4, held_by(6, 3, WIDTHS[4]))
         finish(5, own_tile(5))
         finish(6, own_tile(6))

@@ -25,7 +25,7 @@ QUADRANT = 32
 
 WIDTHS = [512] * 2 + [256] * 3 + [128] * 2
 SHARED = range(2, 5)
-ON_VECTOR = {1: 176, 2: 112, 3: 80, 4: 112, 6: 80}
+ON_VECTOR = {1: 208, 2: 112, 3: 80, 4: 80, 6: 64}
 AHEAD = {2: 2, 3: 2, 4: 1}
 FIRST = 32
 OVERLAP = 16
@@ -84,8 +84,6 @@ def tile_list_tabgate_bias_kernel(tc, tab_words, tab_scales, w4_words, w4_scales
         for r in range(4):
             nc.sync.dma_start(out=w4_plane[r:P:QUADRANT, :], in_=w4_rows[r:SCALE_ROWS:4, :])
         nc.sync.dma_start(out=w4_codes[:], in_=w4_words[0].bitcast(I32))
-        with nc.allow_non_contiguous_dma(reason="one bias value a partition"):
-            nc.sync.dma_start(out=bias[:], in_=b.rearrange("(p o) -> p o", o=1))
         nc.sync.dma_start(out=gates[:], in_=gT)
         nc.sync.dma_start(out=u_raw[:], in_=u.rearrange("(p t) n -> p t n", t=PACK))
         for i in range(SHARED.start):
@@ -93,6 +91,8 @@ def tile_list_tabgate_bias_kernel(tc, tab_words, tab_scales, w4_words, w4_scales
         nc.vector.tensor_copy(picked_rows[:], tab_rows[:].bitcast(U8).indirect(offsets[:]))
         for r in range(4):
             nc.sync.dma_start(out=picked_plane[r:P:QUADRANT, :], in_=picked_rows[STAGED + r : P : 4, :].bitcast(I32))
+        with nc.allow_non_contiguous_dma(reason="one bias value a partition"):
+            nc.sync.dma_start(out=bias[:], in_=b.rearrange("(p o) -> p o", o=1))
         for row in range(max(AHEAD.values())):
             width = sum(WIDTHS[i] for i in SHARED if AHEAD[i] > row)
             load_c(middle_rows[:, row : row + 1, 0:width], c_rows[:, row : row + 1, base : base + width])

@@ -30,7 +30,7 @@ AHEAD = {2: 2, 3: 2, 4: 1}
 FIRST = 32
 OVERLAP = 16
 PAD = 16
-BANKS = 3
+BANKS = 2
 
 
 def tile_list_tabgate_bias_kernel(tc, tab_words, tab_scales, w4_words, w4_scales, c, u, gT, b, offs, out):
@@ -176,7 +176,6 @@ def tile_list_tabgate_bias_kernel(tc, tab_words, tab_scales, w4_words, w4_scales
         round_chunk(0)
         multiply(0)
         open_bank(1)
-        open_bank(2)
         round_chunk(1)
         multiply(1)
         open_bank(6)
@@ -191,9 +190,9 @@ def tile_list_tabgate_bias_kernel(tc, tab_words, tab_scales, w4_words, w4_scales
         multiply(4)
         finish(3, own_tile(3))
         round_chunk(5)
-        multiply(5)
         round_chunk(6)
-        finish(4, own_tile(4))
+        multiply(5)
         multiply(6)
+        finish(4, own_tile(4))
         finish(5, own_tile(5))
         finish(6, own_tile(6))

@@ -28,8 +28,8 @@ SHARED = range(2, 5)
 ON_VECTOR = {1: 208, 2: 112, 3: 80, 4: 80, 6: 64}
 AHEAD = {2: 2, 3: 2, 4: 1}
 FIRST = 32
-OVERLAP = 16
-PAD = 16
+OVERLAP = 64
+PAD = 64
 BANKS = 2
 
 
@@ -42,28 +42,28 @@ def tile_list_tabgate_bias_kernel(tc, tab_words, tab_scales, w4_words, w4_scales
         keep = ctx.enter_context(tc.tile_pool(name="keep", bufs=1))
         psum = ctx.enter_context(tc.psum_pool(name="psum", bufs=1))
 
-        offsets = keep.tile([P, S // PER_COL], U16, name="offsets")
-        tab_rows = keep.tile([P, T // 4], I32, name="tab_rows", align_bytes=64)
-        picked_plane = keep.tile([P, S // 4], I32, name="picked_plane", align_bytes=64)
-        w4_plane = keep.tile([P, M // 4], I32, name="w4_plane", align_bytes=64)
-        tab_codes = keep.tile([P, T], I32, name="tab_codes", align_bytes=64)
-        w4_codes = keep.tile([P, M // 2], I32, name="w4_codes", align_bytes=64)
-        u_raw = keep.tile([P, PACK, M], F32, name="u_raw")
-        bias = keep.tile([P, 1], F32, name="bias")
-        gates = keep.tile([P, T], F32, name="gates")
+        offsets = keep.tile([P, S // PER_COL], U16, name="offsets", align_bytes=256)
+        tab_rows = keep.tile([P, T // 4], I32, name="tab_rows", align_bytes=256)
+        picked_plane = keep.tile([P, S // 4], I32, name="picked_plane", align_bytes=256)
+        w4_plane = keep.tile([P, M // 4], I32, name="w4_plane", align_bytes=256)
+        tab_codes = keep.tile([P, T], I32, name="tab_codes", align_bytes=256)
+        w4_codes = keep.tile([P, M // 2], I32, name="w4_codes", align_bytes=256)
+        u_raw = keep.tile([P, PACK, M], F32, name="u_raw", align_bytes=256)
+        bias = keep.tile([P, 1], F32, name="bias", align_bytes=256)
+        gates = keep.tile([P, T], F32, name="gates", align_bytes=256)
         base, span = starts[SHARED.start], starts[SHARED.stop] - starts[SHARED.start]
         ahead = WIDTHS[SHARED.start - 1] - OVERLAP
-        middle = keep.tile([P, ahead + PACK * (span + PAD)], F32, name="middle")
+        middle = keep.tile([P, ahead + PACK * (span + PAD)], F32, name="middle", align_bytes=256)
         middle_rows = middle[:, ahead:].rearrange("p (t j) -> p t j", t=PACK)
         c_raw = [
             middle_rows[:, :, starts[i] - base : starts[i + 1] - base]
             if i in SHARED
-            else keep.tile([P, PACK, WIDTHS[i] + PAD], F32, name="landing%d" % i)[:, :, 0 : WIDTHS[i]]
+            else keep.tile([P, PACK, WIDTHS[i] + PAD], F32, name="landing%d" % i, align_bytes=256)[:, :, 0 : WIDTHS[i]]
             for i in chunks
         ]
-        picked_rows = keep.tile([P, S], U8, name="picked_rows", align_bytes=64)
-        picked_codes = keep.tile([P, S], U32, name="picked_codes", align_bytes=64)
-        picked_gates = keep.tile([P, S], F32, name="picked_gates")
+        picked_rows = keep.tile([P, S], U8, name="picked_rows", align_bytes=256)
+        picked_codes = keep.tile([P, S], U32, name="picked_codes", align_bytes=256)
+        picked_gates = keep.tile([P, S], F32, name="picked_gates", align_bytes=256)
 
         nc.vector.memset(w4_plane[:], 0)
         nc.vector.memset(tab_rows[0:STAGED, :], 0)
@@ -109,10 +109,10 @@ def tile_list_tabgate_bias_kernel(tc, tab_words, tab_scales, w4_words, w4_scales
                 in_=raw[:, :, lo:hi].rearrange("p t (a i) -> p a t i", i=2),
             )
 
-        codes = keep.tile([P, M + S], U32, name="codes", align_bytes=64)
-        plane = keep.tile([P, M + S], U8, name="plane", align_bytes=64)
-        u_grouped = keep.tile([P, M, PACK], BF16, name="u_grouped", align_bytes=64)
-        grouped = [keep.tile([P, WIDTHS[i], PACK], BF16, name="grouped%d" % i, align_bytes=64) for i in chunks]
+        codes = keep.tile([P, M + S], U32, name="codes", align_bytes=256)
+        plane = keep.tile([P, M + S], U8, name="plane", align_bytes=256)
+        u_grouped = keep.tile([P, M, PACK], BF16, name="u_grouped", align_bytes=256)
+        grouped = [keep.tile([P, WIDTHS[i], PACK], BF16, name="grouped%d" % i, align_bytes=256) for i in chunks]
         banks = {}
 
         def quantise(rounded, lo, hi):
@@ -164,7 +164,7 @@ def tile_list_tabgate_bias_kernel(tc, tab_words, tab_scales, w4_words, w4_scales
                 open_bank(i + BANKS)
 
         def own_tile(i):
-            return keep.tile([P, WIDTHS[i]], F32, name="result%d" % i)[:]
+            return keep.tile([P, WIDTHS[i]], F32, name="result%d" % i, align_bytes=256)[:]
 
         def held_by(i, row, width):
             end = ahead + row * (span + PAD) + starts[i] - base + OVERLAP

@@ -22,14 +22,12 @@ PER_COL = 16
 SCALE_ROWS = K // 32
 STAGED = P - SCALE_ROWS
 QUADRANT = 32
+ALIGN = 256
 
 WIDTHS = [512] * 2 + [256] * 3 + [128] * 2
-SHARED = range(2, 5)
-ON_VECTOR = {1: 208, 2: 112, 3: 80, 4: 80, 6: 64}
-AHEAD = {2: 2, 3: 2, 4: 1}
-FIRST = 32
-OVERLAP = 64
-PAD = 64
+ON_VECTOR = [48, 224, 0, 96, 128, 0, 80]
+HELD_BY = {1: 2, 3: 4, 4: 6}
+PAD = ALIGN // 4
 BANKS = 2
 
 
@@ -42,28 +40,27 @@ def tile_list_tabgate_bias_kernel(tc, tab_words, tab_scales, w4_words, w4_scales
         keep = ctx.enter_context(tc.tile_pool(name="keep", bufs=1))
         psum = ctx.enter_context(tc.psum_pool(name="psum", bufs=1))
 
-        offsets = keep.tile([P, S // PER_COL], U16, name="offsets", align_bytes=256)
-        tab_rows = keep.tile([P, T // 4], I32, name="tab_rows", align_bytes=256)
-        picked_plane = keep.tile([P, S // 4], I32, name="picked_plane", align_bytes=256)
-        w4_plane = keep.tile([P, M // 4], I32, name="w4_plane", align_bytes=256)
-        tab_codes = keep.tile([P, T], I32, name="tab_codes", align_bytes=256)
-        w4_codes = keep.tile([P, M // 2], I32, name="w4_codes", align_bytes=256)
-        u_raw = keep.tile([P, PACK, M], F32, name="u_raw", align_bytes=256)
-        bias = keep.tile([P, 1], F32, name="bias", align_bytes=256)
-        gates = keep.tile([P, T], F32, name="gates", align_bytes=256)
-        base, span = starts[SHARED.start], starts[SHARED.stop] - starts[SHARED.start]
-        ahead = WIDTHS[SHARED.start - 1] - OVERLAP
-        middle = keep.tile([P, ahead + PACK * (span + PAD)], F32, name="middle", align_bytes=256)
-        middle_rows = middle[:, ahead:].rearrange("p (t j) -> p t j", t=PACK)
-        c_raw = [
-            middle_rows[:, :, starts[i] - base : starts[i + 1] - base]
-            if i in SHARED
-            else keep.tile([P, PACK, WIDTHS[i] + PAD], F32, name="landing%d" % i, align_bytes=256)[:, :, 0 : WIDTHS[i]]
-            for i in chunks
-        ]
-        picked_rows = keep.tile([P, S], U8, name="picked_rows", align_bytes=256)
-        picked_codes = keep.tile([P, S], U32, name="picked_codes", align_bytes=256)
-        picked_gates = keep.tile([P, S], F32, name="picked_gates", align_bytes=256)
+        def kept(name, shape, dtype):
+            return keep.tile(shape, dtype, name=name, align_bytes=ALIGN)
+
+        offsets = kept("offsets", [P, S // PER_COL], U16)
+        tab_rows = kept("tab_rows", [P, T // 4], I32)
+        picked_plane = kept("picked_plane", [P, S // 4], I32)
+        w4_plane = kept("w4_plane", [P, M // 4], I32)
+        tab_codes = kept("tab_codes", [P, T], I32)
+        w4_codes = kept("w4_codes", [P, M // 2], I32)
+        u_raw = kept("u_raw", [P, PACK, M], F32)
+        bias = kept("bias", [P, 1], F32)
+        gates = kept("gates", [P, T], F32)
+        landing = [kept("landing%d" % i, [P, PACK * (WIDTHS[i] + PAD)], F32) for i in chunks]
+        c_raw = [landing[i][:].rearrange("p (t j) -> p t j", t=PACK)[:, :, 0 : WIDTHS[i]] for i in chunks]
+        picked_rows = kept("picked_rows", [P, S], U8)
+        picked_codes = kept("picked_codes", [P, S], U32)
+        picked_gates = kept("picked_gates", [P, S], F32)
+        codes = kept("codes", [P, M + S], U32)
+        plane = kept("plane", [P, M + S], U8)
+        u_grouped = kept("u_grouped", [P, M, PACK], BF16)
+        grouped = [kept("grouped%d" % i, [P, WIDTHS[i], PACK], BF16) for i in chunks]
 
         nc.vector.memset(w4_plane[:], 0)
         nc.vector.memset(tab_rows[0:STAGED, :], 0)
@@ -72,11 +69,8 @@ def tile_list_tabgate_bias_kernel(tc, tab_words, tab_scales, w4_words, w4_scales
         w4_rows = w4_scales[0].bitcast(I32)
         c_rows = c.rearrange("(p t) j -> p t j", t=PACK)
 
-        def load_c(tile_rows, hbm_rows):
-            nc.sync.dma_start(
-                out=tile_rows.rearrange("p t (a i) -> p t a i", i=2),
-                in_=hbm_rows.rearrange("p t (a i) -> p t a i", i=2),
-            )
+        def load_c(i):
+            nc.sync.dma_start(out=c_raw[i], in_=c_rows[:, :, starts[i] : starts[i + 1]])
 
         nc.sync.dma_start(out=tab_rows[STAGED:P, :], in_=tab_scales[0].bitcast(I32))
         nc.sync.dma_start(offsets[:], offs)
@@ -86,34 +80,24 @@ def tile_list_tabgate_bias_kernel(tc, tab_words, tab_scales, w4_words, w4_scales
         nc.sync.dma_start(out=w4_codes[:], in_=w4_words[0].bitcast(I32))
         nc.sync.dma_start(out=gates[:], in_=gT)
         nc.sync.dma_start(out=u_raw[:], in_=u.rearrange("(p t) n -> p t n", t=PACK))
-        for i in range(SHARED.start):
-            load_c(c_raw[i], c_rows[:, :, starts[i] : starts[i + 1]])
+        load_c(0)
+        load_c(1)
         nc.vector.tensor_copy(picked_rows[:], tab_rows[:].bitcast(U8).indirect(offsets[:]))
         for r in range(4):
             nc.sync.dma_start(out=picked_plane[r:P:QUADRANT, :], in_=picked_rows[STAGED + r : P : 4, :].bitcast(I32))
         with nc.allow_non_contiguous_dma(reason="one bias value a partition"):
             nc.sync.dma_start(out=bias[:], in_=b.rearrange("(p o) -> p o", o=1))
-        for row in range(max(AHEAD.values())):
-            width = sum(WIDTHS[i] for i in SHARED if AHEAD[i] > row)
-            load_c(middle_rows[:, row : row + 1, 0:width], c_rows[:, row : row + 1, base : base + width])
-        for i in chunks[SHARED.start :]:
-            rows = slice(AHEAD.get(i, 0), PACK)
-            load_c(c_raw[i][:, rows, :], c_rows[:, rows, starts[i] : starts[i + 1]])
+        for i in chunks[2:]:
+            load_c(i)
 
         nc.vector.tensor_copy(picked_codes[:], tab_codes[:].bitcast(U32).indirect(offsets[:]))
         nc.vector.tensor_copy(picked_gates[:], gates[:].indirect(offsets[:]))
 
-        def round_columns(engine_copy, grouped, raw, lo, hi):
+        def round_columns(engine_copy, rounded, raw, lo, hi):
             engine_copy(
-                out=grouped[:, lo:hi, :].rearrange("p (a i) t -> p a t i", i=2),
+                out=rounded[:, lo:hi, :].rearrange("p (a i) t -> p a t i", i=2),
                 in_=raw[:, :, lo:hi].rearrange("p t (a i) -> p a t i", i=2),
             )
-
-        codes = keep.tile([P, M + S], U32, name="codes", align_bytes=256)
-        plane = keep.tile([P, M + S], U8, name="plane", align_bytes=256)
-        u_grouped = keep.tile([P, M, PACK], BF16, name="u_grouped", align_bytes=256)
-        grouped = [keep.tile([P, WIDTHS[i], PACK], BF16, name="grouped%d" % i, align_bytes=256) for i in chunks]
-        banks = {}
 
         def quantise(rounded, lo, hi):
             nc.vector.quantize_mx(
@@ -121,6 +105,8 @@ def tile_list_tabgate_bias_kernel(tc, tab_words, tab_scales, w4_words, w4_scales
                 scales=plane[:, lo:hi],
                 in_=rounded[:].rearrange("p j t -> p (j t)"),
             )
+
+        banks = {}
 
         def open_bank(i):
             banks[i] = psum.tile([P, WIDTHS[i]], F32, name="bank%d" % i, tag="bank%d" % (i % BANKS if i < last else BANKS))
@@ -135,11 +121,9 @@ def tile_list_tabgate_bias_kernel(tc, tab_words, tab_scales, w4_words, w4_scales
                 stop=False,
             )
 
-        def round_chunk(i, first=0):
-            on_scalar = WIDTHS[i] - ON_VECTOR.get(i, 0)
-            if first > 0:
-                round_columns(nc.scalar.copy, grouped[i], c_raw[i], 0, first)
-            round_columns(nc.scalar.copy, grouped[i], c_raw[i], first, on_scalar)
+        def round_chunk(i):
+            on_scalar = WIDTHS[i] - ON_VECTOR[i]
+            round_columns(nc.scalar.copy, grouped[i], c_raw[i], 0, on_scalar)
             if on_scalar < WIDTHS[i]:
                 round_columns(nc.vector.tensor_copy, grouped[i], c_raw[i], on_scalar, WIDTHS[i])
 
@@ -156,19 +140,13 @@ def tile_list_tabgate_bias_kernel(tc, tab_words, tab_scales, w4_words, w4_scales
                 stop=True,
             )
 
-        def finish(i, result):
+        def finish(i):
+            result = landing[HELD_BY[i]][:, 0 : WIDTHS[i]] if i in HELD_BY else kept("result%d" % i, [P, WIDTHS[i]], F32)[:]
             cols = slice(starts[i], starts[i + 1])
             nc.vector.scalar_tensor_tensor(out=result, in0=banks[i][:], scalar=bias[:], in1=picked_gates[:, cols], op0=ADD, op1=MULT)
             nc.sync.dma_start(out=out[:, cols], in_=result)
             if i + BANKS < last:
                 open_bank(i + BANKS)
-
-        def own_tile(i):
-            return keep.tile([P, WIDTHS[i]], F32, name="result%d" % i, align_bytes=256)[:]
-
-        def held_by(i, row, width):
-            end = ahead + row * (span + PAD) + starts[i] - base + OVERLAP
-            return middle[:, end - width : end]
 
         open_bank(0)
         round_columns(nc.scalar.copy, u_grouped, u_raw, 0, M)
@@ -178,21 +156,21 @@ def tile_list_tabgate_bias_kernel(tc, tab_words, tab_scales, w4_words, w4_scales
         open_bank(1)
         round_chunk(1)
         multiply(1)
-        open_bank(6)
-        finish(0, own_tile(0))
+        open_bank(last)
+        finish(0)
         round_chunk(2)
         round_chunk(3)
         multiply(2)
-        finish(1, held_by(2, 0, WIDTHS[1]))
+        finish(1)
         multiply(3)
         round_chunk(4)
-        finish(2, own_tile(2))
+        finish(2)
         multiply(4)
-        finish(3, own_tile(3))
+        finish(3)
         round_chunk(5)
         round_chunk(6)
         multiply(5)
         multiply(6)
-        finish(4, own_tile(4))
-        finish(5, own_tile(5))
-        finish(6, own_tile(6))
+        finish(4)
+        finish(5)
+        finish(6)

@@ -25,7 +25,7 @@ QUADRANT = 32
 ALIGN = 256
 
 WIDTHS = [512] * 2 + [256] * 3 + [128] * 2
-ON_VECTOR = [48, 224, 0, 96, 128, 0, 80]
+ON_VECTOR = [0, 0, 0, 0, 0, 0, 64]
 HELD_BY = {1: 2, 3: 4, 4: 6}
 PAD = ALIGN // 4
 BANKS = 2

@@ -25,7 +25,7 @@ QUADRANT = 32
 ALIGN = 256
 
 WIDTHS = [512] * 2 + [256] * 3 + [128] * 2
-ON_VECTOR = [0, 0, 0, 0, 0, 0, 64]
+ON_VECTOR = [0, 192, 0, 0, 64, 0, 0]
 HELD_BY = {1: 2, 3: 4, 4: 6}
 PAD = ALIGN // 4
 BANKS = 2
@@ -159,9 +159,9 @@ def tile_list_tabgate_bias_kernel(tc, tab_words, tab_scales, w4_words, w4_scales
         open_bank(last)
         finish(0)
         round_chunk(2)
-        round_chunk(3)
         multiply(2)
         finish(1)
+        round_chunk(3)
         multiply(3)
         round_chunk(4)
         finish(2)

@@ -27,7 +27,7 @@ ALIGN = 256
 WIDTHS = [512] * 2 + [256] * 3 + [128] * 2
 ON_VECTOR = [0, 192, 0, 0, 64, 0, 0]
 HELD_BY = {1: 2, 3: 4, 4: 6}
-PAD = ALIGN // 4
+PAD = 0
 BANKS = 2
 
 

@@ -25,10 +25,9 @@ QUADRANT = 32
 ALIGN = 256
 
 WIDTHS = [512] * 2 + [256] * 3 + [128] * 2
-ON_VECTOR = [0, 192, 0, 0, 64, 0, 0]
-HELD_BY = {1: 2, 3: 4, 4: 6}
-PAD = 0
-BANKS = 2
+ON_VECTOR = [0, 192, 0, 0, 128, 0, 0]
+HELD_BY = {1: (2, 0), 2: (4, 0), 3: (4, 1), 4: (6, 0)}
+BANKS = 3
 
 
 def tile_list_tabgate_bias_kernel(tc, tab_words, tab_scales, w4_words, w4_scales, c, u, gT, b, offs, out):
@@ -52,8 +51,8 @@ def tile_list_tabgate_bias_kernel(tc, tab_words, tab_scales, w4_words, w4_scales
         u_raw = kept("u_raw", [P, PACK, M], F32)
         bias = kept("bias", [P, 1], F32)
         gates = kept("gates", [P, T], F32)
-        landing = [kept("landing%d" % i, [P, PACK * (WIDTHS[i] + PAD)], F32) for i in chunks]
-        c_raw = [landing[i][:].rearrange("p (t j) -> p t j", t=PACK)[:, :, 0 : WIDTHS[i]] for i in chunks]
+        landing = [kept("landing%d" % i, [P, PACK * WIDTHS[i]], F32) for i in chunks]
+        c_raw = [landing[i][:].rearrange("p (t j) -> p t j", t=PACK) for i in chunks]
         picked_rows = kept("picked_rows", [P, S], U8)
         picked_codes = kept("picked_codes", [P, S], U32)
         picked_gates = kept("picked_gates", [P, S], F32)
@@ -141,7 +140,11 @@ def tile_list_tabgate_bias_kernel(tc, tab_words, tab_scales, w4_words, w4_scales
             )
 
         def finish(i):
-            result = landing[HELD_BY[i]][:, 0 : WIDTHS[i]] if i in HELD_BY else kept("result%d" % i, [P, WIDTHS[i]], F32)[:]
+            if i in HELD_BY:
+                holder, slot = HELD_BY[i]
+                result = landing[holder][:, slot * WIDTHS[i] : (slot + 1) * WIDTHS[i]]
+            else:
+                result = kept("result%d" % i, [P, WIDTHS[i]], F32)[:]
             cols = slice(starts[i], starts[i + 1])
             nc.vector.scalar_tensor_tensor(out=result, in0=banks[i][:], scalar=bias[:], in1=picked_gates[:, cols], op0=ADD, op1=MULT)
             nc.sync.dma_start(out=out[:, cols], in_=result)
@@ -156,6 +159,7 @@ def tile_list_tabgate_bias_kernel(tc, tab_words, tab_scales, w4_words, w4_scales
         open_bank(1)
         round_chunk(1)
         multiply(1)
+        open_bank(2)
         open_bank(last)
         finish(0)
         round_chunk(2)
@@ -164,8 +168,8 @@ def tile_list_tabgate_bias_kernel(tc, tab_words, tab_scales, w4_words, w4_scales
         round_chunk(3)
         multiply(3)
         round_chunk(4)
-        finish(2)
         multiply(4)
+        finish(2)
         finish(3)
         round_chunk(5)
         round_chunk(6)

from contextlib import ExitStack

import concourse.mybir as mybir

K, M, T, S = 512, 128, 4096, 2048
FLOPS = 2 * 2 * K * M * S

F32 = mybir.dt.float32
BF16 = mybir.dt.bfloat16
I32 = mybir.dt.int32
U32 = mybir.dt.uint32
U16 = mybir.dt.uint16
U8 = mybir.dt.uint8
FP8X4 = mybir.dt.float8_e4m3fn_x4
FP4X4 = mybir.dt.float4_e2m1fn_x4
ADD = mybir.AluOpType.add
MULT = mybir.AluOpType.mult

P = 128
PACK = 4
PER_COL = 16
SCALE_ROWS = K // 32
STAGED = P - SCALE_ROWS
QUADRANT = 32
ALIGN = 256

WIDTHS = [512] * 2 + [256] * 3 + [128] * 2
ON_VECTOR = [0, 192, 0, 0, 128, 0, 0]
HELD_BY = {1: (2, 0), 2: (4, 0), 3: (4, 1), 4: (6, 0)}
BANKS = 3


def tile_list_tabgate_bias_kernel(tc, tab_words, tab_scales, w4_words, w4_scales, c, u, gT, b, offs, out):
    nc = tc.nc
    chunks = range(len(WIDTHS))
    last = len(WIDTHS) - 1
    starts = [sum(WIDTHS[:i]) for i in range(len(WIDTHS) + 1)]
    with ExitStack() as ctx:
        keep = ctx.enter_context(tc.tile_pool(name="keep", bufs=1))
        psum = ctx.enter_context(tc.psum_pool(name="psum", bufs=1))

        def kept(name, shape, dtype):
            return keep.tile(shape, dtype, name=name, align_bytes=ALIGN)

        offsets = kept("offsets", [P, S // PER_COL], U16)
        tab_rows = kept("tab_rows", [P, T // 4], I32)
        picked_plane = kept("picked_plane", [P, S // 4], I32)
        w4_plane = kept("w4_plane", [P, M // 4], I32)
        tab_codes = kept("tab_codes", [P, T], I32)
        w4_codes = kept("w4_codes", [P, M // 2], I32)
        u_raw = kept("u_raw", [P, PACK, M], F32)
        bias = kept("bias", [P, 1], F32)
        gates = kept("gates", [P, T], F32)
        landing = [kept("landing%d" % i, [P, PACK * WIDTHS[i]], F32) for i in chunks]
        c_raw = [landing[i][:].rearrange("p (t j) -> p t j", t=PACK) for i in chunks]
        picked_rows = kept("picked_rows", [P, S], U8)
        picked_codes = kept("picked_codes", [P, S], U32)
        picked_gates = kept("picked_gates", [P, S], F32)
        codes = kept("codes", [P, M + S], U32)
        plane = kept("plane", [P, M + S], U8)
        u_grouped = kept("u_grouped", [P, M, PACK], BF16)
        grouped = [kept("grouped%d" % i, [P, WIDTHS[i], PACK], BF16) for i in chunks]

        nc.vector.memset(w4_plane[:], 0)
        nc.vector.memset(tab_rows[0:STAGED, :], 0)
        nc.vector.memset(picked_plane[:], 0)

        w4_rows = w4_scales[0].bitcast(I32)
        c_rows = c.rearrange("(p t) j -> p t j", t=PACK)

        def load_c(i):
            nc.sync.dma_start(out=c_raw[i], in_=c_rows[:, :, starts[i] : starts[i + 1]])

        nc.sync.dma_start(out=tab_rows[STAGED:P, :], in_=tab_scales[0].bitcast(I32))
        nc.sync.dma_start(offsets[:], offs)
        nc.sync.dma_start(out=tab_codes[:], in_=tab_words[0].rearrange("p t i -> p (t i)").bitcast(I32))
        for r in range(4):
            nc.sync.dma_start(out=w4_plane[r:P:QUADRANT, :], in_=w4_rows[r:SCALE_ROWS:4, :])
        nc.sync.dma_start(out=w4_codes[:], in_=w4_words[0].bitcast(I32))
        nc.sync.dma_start(out=gates[:], in_=gT)
        nc.sync.dma_start(out=u_raw[:], in_=u.rearrange("(p t) n -> p t n", t=PACK))
        load_c(0)
        load_c(1)
        nc.vector.tensor_copy(picked_rows[:], tab_rows[:].bitcast(U8).indirect(offsets[:]))
        for r in range(4):
            nc.sync.dma_start(out=picked_plane[r:P:QUADRANT, :], in_=picked_rows[STAGED + r : P : 4, :].bitcast(I32))
        with nc.allow_non_contiguous_dma(reason="one bias value a partition"):
            nc.sync.dma_start(out=bias[:], in_=b.rearrange("(p o) -> p o", o=1))
        for i in chunks[2:]:
            load_c(i)

        nc.vector.tensor_copy(picked_codes[:], tab_codes[:].bitcast(U32).indirect(offsets[:]))
        nc.vector.tensor_copy(picked_gates[:], gates[:].indirect(offsets[:]))

        def round_columns(engine_copy, rounded, raw, lo, hi):
            engine_copy(
                out=rounded[:, lo:hi, :].rearrange("p (a i) t -> p a t i", i=2),
                in_=raw[:, :, lo:hi].rearrange("p t (a i) -> p a t i", i=2),
            )

        def quantise(rounded, lo, hi):
            nc.vector.quantize_mx(
                out=codes[:, lo:hi].bitcast(FP8X4),
                scales=plane[:, lo:hi],
                in_=rounded[:].rearrange("p j t -> p (j t)"),
            )

        banks = {}

        def open_bank(i):
            banks[i] = psum.tile([P, WIDTHS[i]], F32, name="bank%d" % i, tag="bank%d" % (i % BANKS if i < last else BANKS))
            cols = slice(starts[i], starts[i + 1])
            nc.tensor.matmul_mx(
                out=banks[i][:],
                lhsT=w4_codes[:].bitcast(FP4X4),
                lhsT_scale=w4_plane[:].bitcast(U8),
                rhs=picked_codes[:, cols].bitcast(FP8X4),
                rhs_scale=picked_plane[:].bitcast(U8)[:, cols],
                start=True,
                stop=False,
            )

        def round_chunk(i):
            on_scalar = WIDTHS[i] - ON_VECTOR[i]
            round_columns(nc.scalar.copy, grouped[i], c_raw[i], 0, on_scalar)
            if on_scalar < WIDTHS[i]:
                round_columns(nc.vector.tensor_copy, grouped[i], c_raw[i], on_scalar, WIDTHS[i])

        def multiply(i):
            lo, hi = M + starts[i], M + starts[i + 1]
            quantise(grouped[i], lo, hi)
            nc.tensor.matmul_mx(
                out=banks[i][:],
                lhsT=codes[:, 0:M].bitcast(FP8X4),
                lhsT_scale=plane[:, 0:M],
                rhs=codes[:, lo:hi].bitcast(FP8X4),
                rhs_scale=plane[:, lo:hi],
                start=False,
                stop=True,
            )

        def finish(i):
            if i in HELD_BY:
                holder, slot = HELD_BY[i]
                result = landing[holder][:, slot * WIDTHS[i] : (slot + 1) * WIDTHS[i]]
            else:
                result = kept("result%d" % i, [P, WIDTHS[i]], F32)[:]
            cols = slice(starts[i], starts[i + 1])
            nc.vector.scalar_tensor_tensor(out=result, in0=banks[i][:], scalar=bias[:], in1=picked_gates[:, cols], op0=ADD, op1=MULT)
            nc.sync.dma_start(out=out[:, cols], in_=result)
            if i + BANKS < last:
                open_bank(i + BANKS)

        open_bank(0)
        round_columns(nc.scalar.copy, u_grouped, u_raw, 0, M)
        quantise(u_grouped, 0, M)
        round_chunk(0)
        multiply(0)
        open_bank(1)
        round_chunk(1)
        multiply(1)
        open_bank(2)
        open_bank(last)
        finish(0)
        round_chunk(2)
        multiply(2)
        finish(1)
        round_chunk(3)
        multiply(3)
        round_chunk(4)
        multiply(4)
        finish(2)
        finish(3)
        round_chunk(5)
        round_chunk(6)
        multiply(5)
        multiply(6)
        finish(4)
        finish(5)
        finish(6)
